import numpy as np
import ml_dtypes


def mxq(x, axis, fmt="e4m3"):
    dtype, down = {"e4m3": (ml_dtypes.float8_e4m3fn, 7), "e5m2": (ml_dtypes.float8_e5m2, 14)}[fmt]
    v = np.moveaxis(np.asarray(x, np.float32).astype(ml_dtypes.bfloat16).astype(np.float64), axis, -1)
    blocks = v.reshape(v.shape[:-1] + (-1, 32))
    amax = np.abs(blocks).max(-1, keepdims=True)
    byte = np.maximum(np.where(amax > 0, np.frexp(amax)[1] - 1 + 127, 0) - down, 1)
    scale = np.exp2(byte - 127.0)
    codes = (blocks / scale).astype(np.float32).astype(dtype).astype(np.float64)
    return np.moveaxis((codes * scale).reshape(v.shape), -1, axis)


WIDE = False


def mx_kscale(k):
    if not WIDE:
        return np.ones(k)
    levels = np.array([10, -10, 5, -5, 0])
    if k % 512:
        return np.exp2(np.random.permutation(np.resize(levels, k // 32))).repeat(32)
    a = np.empty((k // 512, 16))
    for p in range(k // 512):
        a[p, :8] = np.random.permutation(np.resize(levels, 8))
        for g in range(8):
            far = levels[np.abs(levels - a[p, g]) >= 10]
            a[p, g + 8] = far[np.random.randint(len(far))]
    return np.exp2(a.ravel()).repeat(32)


def f64(x):
    return np.asarray(x).astype(np.float64)


def striped(idx):
    return np.tile(idx.reshape(-1, 16).T, (8, 1)).astype(np.uint16)


def unstriped(offs):
    return offs[:16].T.reshape(-1).astype(np.int64)


def pack_weight(w):
    k, n = w.shape
    w = f64(np.asarray(w, np.float32).astype(ml_dtypes.bfloat16)).reshape(k // 32, 32, n)
    amax = np.abs(w).max(1)
    byte = np.clip(np.where(amax > 0, np.frexp(amax)[1] - 1 + 127 - 7, 1), 1, 254)
    scaled = (w * np.exp2(127.0 - byte)[:, None, :]).reshape(k, n).astype(np.float32)
    words = np.ascontiguousarray(scaled.reshape(k // 512, 128, 4, n).transpose(0, 1, 3, 2)).astype(ml_dtypes.float8_e4m3fn).view(np.uint8)
    return words, np.ascontiguousarray(byte.astype(np.uint8).reshape(k // 512, 16, n))


def unpack_weight(words, scales):
    g, p, n, _ = words.shape
    vals = np.ascontiguousarray(words).view(ml_dtypes.float8_e4m3fn).astype(np.float64) * np.repeat(np.exp2(scales.astype(np.float64) - 127.0), 8, axis=1)[..., None]
    return vals.transpose(0, 1, 3, 2).reshape(g * 512, n)


def relu(v):
    return np.maximum(v, 0.0)


K, T, E, C, N = 512, 1024, 8, 256, 128


def by_expert(wq, xq):
    return np.concatenate([wq[e].T @ xq[:, e * C:(e + 1) * C] for e in range(E)], axis=1)


def setup_inputs():
    n = np.random.standard_normal
    s = mx_kscale(K)[:, None]
    first = np.random.permutation(np.repeat(np.arange(E), T // E))
    second = (first + 1 + np.random.permutation(np.repeat(np.arange(E - 1), -(-T // (E - 1)))[:T])) % E
    while np.bincount(second, minlength=E).max() != T // E:
        load = np.bincount(second, minlength=E); hi, lo = int(load.argmax()), int(load.argmin())
        t = np.flatnonzero((second == hi) & (first != lo))[0]; second[t] = lo
    slot_token = np.empty(E * C, np.int64); pos = np.empty((2, T), np.int64); fill = np.zeros(E, np.int64)
    place = np.stack([np.random.permutation(C) for _ in range(E)])
    for r, deal in enumerate((first, second)):
        for t in np.random.permutation(T):
            e = deal[t]; j = e * C + place[e, fill[e]]; fill[e] += 1; slot_token[j] = t; pos[r, t] = j
    g = np.random.uniform(0.2, 0.8, T)
    packed = [pack_weight(m) for m in n((E, K, N)) / np.sqrt(K) / s[None]]
    return {
        "xT": (n((K, T)) * s).astype(np.float32),
        "w_words": np.stack([m[0] for m in packed]),
        "w_scales": np.stack([m[1] for m in packed]),
        "b": (0.3 * n((N, E))).astype(np.float32),
        "gate": np.stack([np.tile(g, (N, 1)), np.tile(1.0 - g, (N, 1))]).astype(np.float32),
        "offs": striped(slot_token),
        "pos1": striped(pos[0]),
        "pos2": striped(pos[1]),
    }


def reference(xT, w_words, w_scales, b, gate, offs, pos1, pos2):
    idx = unstriped(offs)
    xq = mxq(f64(xT)[:, idx], 0, "e4m3")
    w = np.stack([unpack_weight(w_words[e], w_scales[e]) for e in range(E)])
    y = by_expert(w, xq)
    y = relu(y + np.repeat(f64(b), C, axis=1))
    return f64(gate[0]) * y[:, unstriped(pos1)] + f64(gate[1]) * y[:, unstriped(pos2)]

@@ -1,0 +1,140 @@
+from contextlib import ExitStack
+
+import concourse.mybir as mybir
+
+K, T, E, C, N = 512, 1024, 8, 256, 128
+SLOTS = E * C
+P = 128
+PACK = 4
+
+F32 = mybir.dt.float32
+BF16 = mybir.dt.bfloat16
+U32 = mybir.dt.uint32
+I32 = mybir.dt.int32
+U16 = mybir.dt.uint16
+U8 = mybir.dt.uint8
+FP8X4 = mybir.dt.float8_e4m3fn_x4
+RELU = mybir.ActivationFunctionType.Relu
+ADD = mybir.AluOpType.add
+MAX = mybir.AluOpType.max
+MULT = mybir.AluOpType.mult
+
+FLOPS = 2 * K * N * SLOTS
+
+LOADS = ((0, 256), (256, 256), (512, 384), (896, 128))
+CHUNKS = ((0, 0, 256, 144), (1, 256, 256, 144), (2, 512, 256, 144), (2, 768, 128, 80), (3, 896, 128, 88))
+BYTE_PIECES = ((0, 768), (768, 768), (1536, 512))
+WORD_PIECES = (((0, 768),), ((768, 768),), ((1536, 256), (1792, 256)))
+TOKEN_PIECES = ((0, 640), (640, 256), (896, 128))
+
+
+def tile_routed_moe_kernel(tc, xT, w_words, w_scales, b, gate, offs, pos1, pos2, out):
+    nc = tc.nc
+    with ExitStack() as ctx:
+        keep = ctx.enter_context(tc.tile_pool(name="keep", bufs=1))
+        stage = ctx.enter_context(tc.tile_pool(name="stage", bufs=4))
+        psum = ctx.enter_context(tc.psum_pool(name="psum", bufs=8))
+
+        offs_sb = keep.tile([P, SLOTS // 16], U16, name="offs_sb")
+        pos1_sb = keep.tile([P, T // 16], U16, name="pos1_sb")
+        pos2_sb = keep.tile([P, T // 16], U16, name="pos2_sb")
+        x_words = keep.tile([P, T], U32, name="x_words", align_bytes=64)
+        x_scales = keep.tile([P, T], U8, name="x_scales", align_bytes=64)
+        s_words = keep.tile([P, SLOTS], U32, name="s_words", align_bytes=64)
+        s_scales = keep.tile([P, SLOTS], U8, name="s_scales", align_bytes=64)
+        w_sb = keep.tile([P, E, N * PACK], U8, name="w_sb", align_bytes=64)
+        ws_sb = keep.tile([P, E, N], U8, name="ws_sb", align_bytes=64)
+        b_sb = keep.tile([P, E], F32, name="b_sb")
+        gate1_sb = keep.tile([P, T], F32, name="gate1_sb")
+        gate2_sb = keep.tile([P, T], F32, name="gate2_sb")
+        y = keep.tile([P, SLOTS], F32, name="y")
+
+        nc.gpsimd.memset(x_scales[:], 0)
+        nc.vector.memset(ws_sb[:].rearrange("p e n -> p (e n)").bitcast(I32), 0)
+
+        x_rows = xT.rearrange("(p j) t -> p j t", j=PACK)
+        raws = []
+        for t0, n in LOADS:
+            raw = stage.tile([P, PACK, n], F32, name="raw", bufs=len(LOADS))
+            nc.sync.dma_start(out=raw[:], in_=x_rows[:, :, t0 : t0 + n])
+            raws.append(raw)
+            if t0 == 0:
+                nc.sync.dma_start(offs_sb[:], offs)
+        for q in range(4):
+            nc.sync.dma_start(
+                out=ws_sb[32 * q : 32 * q + 4, :, :].bitcast(I32),
+                in_=w_scales[:, 0, 4 * q : 4 * q + 4, :].rearrange("e q n -> q e n").bitcast(I32),
+            )
+        nc.sync.dma_start(out=w_sb[:], in_=w_words.rearrange("e a p n r -> p (e a) (n r)"))
+        nc.sync.dma_start(out=b_sb[:], in_=b)
+        nc.sync.dma_start(pos1_sb[:], pos1)
+        nc.sync.dma_start(out=gate1_sb[:], in_=gate[0])
+        nc.sync.dma_start(pos2_sb[:], pos2)
+        nc.sync.dma_start(out=gate2_sb[:], in_=gate[1])
+
+        def interleave(chunk):
+            load, t0, n, nv = chunk
+            raw, r0 = raws[load], t0 - LOADS[load][0]
+            grouped = stage.tile([P, n, PACK], BF16, name="grouped", bufs=len(CHUNKS), align_bytes=64)
+            nc.vector.tensor_copy(out=grouped[:, 0:nv, :], in_=raw[:, :, r0 : r0 + nv].rearrange("p j n -> p n j"))
+            nc.scalar.copy(out=grouped[:, nv:n, :], in_=raw[:, :, r0 + nv : r0 + n].rearrange("p j n -> p n j"))
+            return grouped
+
+        def quantise(chunk, grouped):
+            load, t0, n, nv = chunk
+            nc.vector.quantize_mx(
+                out=x_words[:, t0 : t0 + n].bitcast(FP8X4),
+                scales=x_scales[:, t0 : t0 + n],
+                in_=grouped[:].rearrange("p n j -> p (n j)"),
+            )
+
+        for load in range(len(LOADS)):
+            chunks = [c for c in CHUNKS if c[0] == load]
+            grouped = [interleave(c) for c in chunks]
+            for c, g in zip(chunks, grouped):
+                quantise(c, g)
+
+        for (b0, bn), words in zip(BYTE_PIECES, WORD_PIECES):
+            nc.vector.tensor_copy(
+                out=s_scales[:, b0 : b0 + bn], in_=x_scales[:].indirect(offs_sb[:, b0 // 16 : (b0 + bn) // 16])
+            )
+            for j0, n in words:
+                nc.vector.tensor_copy(
+                    out=s_words[:, j0 : j0 + n], in_=x_words[:].indirect(offs_sb[:, j0 // 16 : (j0 + n) // 16])
+                )
+                for e in range(j0 // C, (j0 + n) // C):
+                    slots = slice(e * C, (e + 1) * C)
+                    acc = psum.tile([N, C], F32, name="acc")
+                    nc.tensor.matmul_mx(
+                        out=acc[:],
+                        lhsT=w_sb[:, e, :].bitcast(FP8X4),
+                        lhsT_scale=ws_sb[:, e, :],
+                        rhs=s_words[:, slots].bitcast(FP8X4),
+                        rhs_scale=s_scales[:, slots],
+                        start=True,
+                        stop=True,
+                    )
+                    nc.scalar.activation(y[:, slots], acc[:], RELU, bias=b_sb[:, e : e + 1])
+
+        part1 = keep.tile([P, T], F32, name="part1")
+        nc.vector.tensor_tensor(part1[:], y[:].indirect(pos1_sb[:]), gate1_sb[:], MULT)
+
+        def second_part(t0, n):
+            part2 = stage.tile([P, n], F32, name="part2")
+            nc.vector.tensor_tensor(
+                part2[:], y[:].indirect(pos2_sb[:, t0 // 16 : (t0 + n) // 16]), gate2_sb[:, t0 : t0 + n], MULT
+            )
+            return part2
+
+        def add_and_store(t0, n, part2):
+            total = stage.tile([P, n], F32, name="total")
+            nc.vector.tensor_tensor(total[:], part1[:, t0 : t0 + n], part2[:], ADD)
+            nc.sync.dma_start(out=out[:, t0 : t0 + n], in_=total[:])
+
+        waiting = None
+        for t0, n in TOKEN_PIECES:
+            part2 = second_part(t0, n)
+            if waiting is not None:
+                add_and_store(*waiting)
+            waiting = (t0, n, part2)
+        add_and_store(*waiting)

@@ -1,6 +1,7 @@
 from contextlib import ExitStack
 
 import concourse.mybir as mybir
+from concourse.masks import make_identity
 
 K, T, E, C, N = 512, 1024, 8, 256, 128
 SLOTS = E * C
@@ -23,9 +24,10 @@ FLOPS = 2 * K * N * SLOTS
 
 LOADS = ((0, 256), (256, 256), (512, 384), (896, 128))
 CHUNKS = ((0, 0, 256, 144), (1, 256, 256, 144), (2, 512, 256, 144), (2, 768, 128, 80), (3, 896, 128, 88))
-BYTE_PIECES = ((0, 768), (768, 768), (1536, 512))
-WORD_PIECES = (((0, 768),), ((768, 768),), ((1536, 256), (1792, 256)))
-TOKEN_PIECES = ((0, 640), (640, 256), (896, 128))
+WORD_PIECES = ((0, 1024), (1024, 512), (1536, 384), (1920, 128))
+VECTOR_START = 384
+BACK = 128
+TOKEN_PIECES = ((384, 320), (704, 192), (896, 128))
 
 
 def tile_routed_moe_kernel(tc, xT, w_words, w_scales, b, gate, offs, pos1, pos2, out):
@@ -38,18 +40,21 @@ def tile_routed_moe_kernel(tc, xT, w_words, w_scales, b, gate, offs, pos1, pos2,
         offs_sb = keep.tile([P, SLOTS // 16], U16, name="offs_sb")
         pos1_sb = keep.tile([P, T // 16], U16, name="pos1_sb")
         pos2_sb = keep.tile([P, T // 16], U16, name="pos2_sb")
-        x_words = keep.tile([P, T], U32, name="x_words", align_bytes=64)
-        x_scales = keep.tile([P, T], U8, name="x_scales", align_bytes=64)
+        x_words = keep.tile([P, 2 * T], U32, name="x_words", align_bytes=64)
+        x_scales = keep.tile([P, 4 * T], U8, name="x_scales", align_bytes=64)
         s_words = keep.tile([P, SLOTS], U32, name="s_words", align_bytes=64)
         s_scales = keep.tile([P, SLOTS], U8, name="s_scales", align_bytes=64)
         w_sb = keep.tile([P, E, N * PACK], U8, name="w_sb", align_bytes=64)
         ws_sb = keep.tile([P, E, N], U8, name="ws_sb", align_bytes=64)
         b_sb = keep.tile([P, E], F32, name="b_sb")
-        gate1_sb = keep.tile([P, T], F32, name="gate1_sb")
-        gate2_sb = keep.tile([P, T], F32, name="gate2_sb")
+        gates = keep.tile([P, 2, T], F32, name="gates")
+        gate1_sb, gate2_sb = gates[:, 0, :], gates[:, 1, :]
         y = keep.tile([P, SLOTS], F32, name="y")
+        ident = keep.tile([P, P], F32, name="ident")
+        make_identity(nc, ident[:])
 
-        nc.gpsimd.memset(x_scales[:], 0)
+        nc.vector.memset(x_scales[:].bitcast(I32), 0)
+        nc.vector.memset(x_words[:, T : 2 * T].bitcast(I32), 0)
         nc.vector.memset(ws_sb[:].rearrange("p e n -> p (e n)").bitcast(I32), 0)
 
         x_rows = xT.rearrange("(p j) t -> p j t", j=PACK)
@@ -68,9 +73,8 @@ def tile_routed_moe_kernel(tc, xT, w_words, w_scales, b, gate, offs, pos1, pos2,
         nc.sync.dma_start(out=w_sb[:], in_=w_words.rearrange("e a p n r -> p (e a) (n r)"))
         nc.sync.dma_start(out=b_sb[:], in_=b)
         nc.sync.dma_start(pos1_sb[:], pos1)
-        nc.sync.dma_start(out=gate1_sb[:], in_=gate[0])
         nc.sync.dma_start(pos2_sb[:], pos2)
-        nc.sync.dma_start(out=gate2_sb[:], in_=gate[1])
+        nc.sync.dma_start(out=gates[:], in_=gate.rearrange("g n t -> n g t"))
 
         def interleave(chunk):
             load, t0, n, nv = chunk
@@ -94,30 +98,50 @@ def tile_routed_moe_kernel(tc, xT, w_words, w_scales, b, gate, offs, pos1, pos2,
             for c, g in zip(chunks, grouped):
                 quantise(c, g)
 
-        for (b0, bn), words in zip(BYTE_PIECES, WORD_PIECES):
-            nc.vector.tensor_copy(
-                out=s_scales[:, b0 : b0 + bn], in_=x_scales[:].indirect(offs_sb[:, b0 // 16 : (b0 + bn) // 16])
-            )
-            for j0, n in words:
-                nc.vector.tensor_copy(
-                    out=s_words[:, j0 : j0 + n], in_=x_words[:].indirect(offs_sb[:, j0 // 16 : (j0 + n) // 16])
+        nc.vector.tensor_copy(out=s_scales[:], in_=x_scales[:].indirect(offs_sb[:]))
+        for j0, n in WORD_PIECES:
+            window = x_words[:] if n >= T else x_words[:, 0:T]
+            nc.vector.tensor_copy(out=s_words[:, j0 : j0 + n], in_=window.indirect(offs_sb[:, j0 // 16 : (j0 + n) // 16]))
+            for e in range(j0 // C, (j0 + n - 1) // C + 1):
+                lo, hi = max(j0, e * C), min(j0 + n, (e + 1) * C)
+                acc = psum.tile([N, hi - lo], F32, name="bank")
+                nc.tensor.matmul_mx(
+                    out=acc[:],
+                    lhsT=w_sb[:, e, :].bitcast(FP8X4),
+                    lhsT_scale=ws_sb[:, e, :],
+                    rhs=s_words[:, lo:hi].bitcast(FP8X4),
+                    rhs_scale=s_scales[:, lo:hi],
+                    start=True,
+                    stop=True,
                 )
-                for e in range(j0 // C, (j0 + n) // C):
-                    slots = slice(e * C, (e + 1) * C)
-                    acc = psum.tile([N, C], F32, name="acc")
-                    nc.tensor.matmul_mx(
-                        out=acc[:],
-                        lhsT=w_sb[:, e, :].bitcast(FP8X4),
-                        lhsT_scale=ws_sb[:, e, :],
-                        rhs=s_words[:, slots].bitcast(FP8X4),
-                        rhs_scale=s_scales[:, slots],
-                        start=True,
-                        stop=True,
-                    )
-                    nc.scalar.activation(y[:, slots], acc[:], RELU, bias=b_sb[:, e : e + 1])
+                nc.scalar.activation(y[:, lo:hi], acc[:], RELU, bias=b_sb[:, e : e + 1])
 
-        part1 = keep.tile([P, T], F32, name="part1")
-        nc.vector.tensor_tensor(part1[:], y[:].indirect(pos1_sb[:]), gate1_sb[:], MULT)
+        def gated(pos_sb, gate_sb, t0, n, name):
+            part = keep.tile([P, n], F32, name=name)
+            nc.vector.tensor_tensor(part[:], y[:].indirect(pos_sb[:, t0 // 16 : (t0 + n) // 16]), gate_sb[:, t0 : t0 + n], MULT)
+            return part
+
+        blocks = range(0, VECTOR_START, P)
+        first = gated(pos1_sb, gate1_sb, 0, VECTOR_START, "first")
+        turned = [psum.tile([P, P], F32, name="bank") for c0 in blocks]
+        for c0, bank in zip(blocks, turned):
+            nc.tensor.matmul(bank[:], first[:, c0 : c0 + P], ident[:], start=True, stop=False, is_transpose=True)
+        second = gated(pos2_sb, gate2_sb, 0, VECTOR_START, "second")
+        turned_sb = []
+        for c0, bank in zip(blocks, turned):
+            nc.tensor.matmul(bank[:], second[:, c0 : c0 + P], ident[:], start=False, stop=True, is_transpose=True)
+            held = stage.tile([P, P], F32, name="held", bufs=len(blocks))
+            nc.scalar.copy(out=held[:], in_=bank[:])
+            turned_sb.append(held)
+        for t0 in range(0, VECTOR_START, BACK):
+            back = psum.tile([P, BACK], F32, name="bank")
+            for c0 in range(0, BACK, P):
+                nc.tensor.transpose(back[:, c0 : c0 + P], turned_sb[(t0 + c0) // P][:], ident[:])
+            summed = stage.tile([P, BACK], F32, name="summed", bufs=3)
+            nc.scalar.copy(out=summed[:], in_=back[:])
+            nc.sync.dma_start(out=out[:, t0 : t0 + BACK], in_=summed[:])
+
+        part1 = gated(pos1_sb, gate1_sb, VECTOR_START, T - VECTOR_START, "part1")
 
         def second_part(t0, n):
             part2 = stage.tile([P, n], F32, name="part2")
@@ -128,7 +152,7 @@ def tile_routed_moe_kernel(tc, xT, w_words, w_scales, b, gate, offs, pos1, pos2,
 
         def add_and_store(t0, n, part2):
             total = stage.tile([P, n], F32, name="total")
-            nc.vector.tensor_tensor(total[:], part1[:, t0 : t0 + n], part2[:], ADD)
+            nc.vector.tensor_tensor(total[:], part1[:, t0 - VECTOR_START : t0 - VECTOR_START + n], part2[:], ADD)
             nc.sync.dma_start(out=out[:, t0 : t0 + n], in_=total[:])
 
         waiting = None

@@ -22,12 +22,12 @@ MULT = mybir.AluOpType.mult
 
 FLOPS = 2 * K * N * SLOTS
 
-LOADS = ((0, 256), (256, 256), (512, 384), (896, 128))
-CHUNKS = ((0, 0, 256, 144), (1, 256, 256, 144), (2, 512, 256, 144), (2, 768, 128, 80), (3, 896, 128, 88))
-WORD_PIECES = ((0, 1024), (1024, 512), (1536, 384), (1920, 128))
-VECTOR_START = 384
+LOADS = ((0, 256), (256, 256), (512, 256), (768, 128), (896, 128))
+CHUNKS = ((0, 0, 256, 160), (1, 256, 256, 160), (2, 512, 256, 160), (3, 768, 128, 80), (4, 896, 128, 88))
+WORD_PIECES = ((0, 896), (896, 640), (1536, 384), (1920, 128))
+VECTOR_START = 512
 BACK = 128
-TOKEN_PIECES = ((384, 320), (704, 192), (896, 128))
+TOKEN_PIECES = ((512, 256), (768, 128), (896, 128))
 
 
 def tile_routed_moe_kernel(tc, xT, w_words, w_scales, b, gate, offs, pos1, pos2, out):
@@ -63,7 +63,7 @@ def tile_routed_moe_kernel(tc, xT, w_words, w_scales, b, gate, offs, pos1, pos2,
             raw = stage.tile([P, PACK, n], F32, name="raw", bufs=len(LOADS))
             nc.sync.dma_start(out=raw[:], in_=x_rows[:, :, t0 : t0 + n])
             raws.append(raw)
-            if t0 == 0:
+            if t0 == 896:
                 nc.sync.dma_start(offs_sb[:], offs)
         for q in range(4):
             nc.sync.dma_start(
@@ -80,8 +80,14 @@ def tile_routed_moe_kernel(tc, xT, w_words, w_scales, b, gate, offs, pos1, pos2,
             load, t0, n, nv = chunk
             raw, r0 = raws[load], t0 - LOADS[load][0]
             grouped = stage.tile([P, n, PACK], BF16, name="grouped", bufs=len(CHUNKS), align_bytes=64)
-            nc.vector.tensor_copy(out=grouped[:, 0:nv, :], in_=raw[:, :, r0 : r0 + nv].rearrange("p j n -> p n j"))
-            nc.scalar.copy(out=grouped[:, nv:n, :], in_=raw[:, :, r0 + nv : r0 + n].rearrange("p j n -> p n j"))
+            nc.vector.tensor_copy(
+                out=grouped[:, 0:nv, :].rearrange("p (c i) j -> p c j i", i=4),
+                in_=raw[:, :, r0 : r0 + nv].rearrange("p j (c i) -> p c j i", i=4),
+            )
+            nc.scalar.copy(
+                out=grouped[:, nv:n, :].rearrange("p (c i) j -> p c j i", i=4),
+                in_=raw[:, :, r0 + nv : r0 + n].rearrange("p j (c i) -> p c j i", i=4),
+            )
             return grouped
 
         def quantise(chunk, grouped):
@@ -100,7 +106,7 @@ def tile_routed_moe_kernel(tc, xT, w_words, w_scales, b, gate, offs, pos1, pos2,
 
         nc.vector.tensor_copy(out=s_scales[:], in_=x_scales[:].indirect(offs_sb[:]))
         for j0, n in WORD_PIECES:
-            window = x_words[:] if n >= T else x_words[:, 0:T]
+            window = x_words[:] if n > 768 else x_words[:, 0:T]
             nc.vector.tensor_copy(out=s_words[:, j0 : j0 + n], in_=window.indirect(offs_sb[:, j0 // 16 : (j0 + n) // 16]))
             for e in range(j0 // C, (j0 + n - 1) // C + 1):
                 lo, hi = max(j0, e * C), min(j0 + n, (e + 1) * C)
@@ -114,7 +120,10 @@ def tile_routed_moe_kernel(tc, xT, w_words, w_scales, b, gate, offs, pos1, pos2,
                     start=True,
                     stop=True,
                 )
-                nc.scalar.activation(y[:, lo:hi], acc[:], RELU, bias=b_sb[:, e : e + 1])
+                if hi == WORD_PIECES[-1][0]:
+                    nc.vector.tensor_scalar(y[:, lo:hi], acc[:], b_sb[:, e : e + 1], 0.0, ADD, MAX)
+                else:
+                    nc.scalar.activation(y[:, lo:hi], acc[:], RELU, bias=b_sb[:, e : e + 1])
 
         def gated(pos_sb, gate_sb, t0, n, name):
             part = keep.tile([P, n], F32, name=name)
@@ -137,9 +146,9 @@ def tile_routed_moe_kernel(tc, xT, w_words, w_scales, b, gate, offs, pos1, pos2,
             back = psum.tile([P, BACK], F32, name="bank")
             for c0 in range(0, BACK, P):
                 nc.tensor.transpose(back[:, c0 : c0 + P], turned_sb[(t0 + c0) // P][:], ident[:])
-            summed = stage.tile([P, BACK], F32, name="summed", bufs=3)
+            summed = stage.tile([P, BACK], F32, name="summed", bufs=4)
             nc.scalar.copy(out=summed[:], in_=back[:])
-            nc.sync.dma_start(out=out[:, t0 : t0 + BACK], in_=summed[:])
+            nc.scalar.dma_start(out=out[:, t0 : t0 + BACK], in_=summed[:])
 
         part1 = gated(pos1_sb, gate1_sb, VECTOR_START, T - VECTOR_START, "part1")
 

@@ -23,7 +23,8 @@ MULT = mybir.AluOpType.mult
 FLOPS = 2 * K * N * SLOTS
 
 LOADS = ((0, 256), (256, 256), (512, 256), (768, 128), (896, 128))
-CHUNKS = ((0, 0, 256, 160), (1, 256, 256, 160), (2, 512, 256, 160), (3, 768, 128, 80), (4, 896, 128, 88))
+CHUNKS = ((0, 256, 176), (256, 256, 144), (512, 256, 160), (768, 128, 80), (896, 128, 88))
+EARLY_VECTOR, EARLY_SCALAR = 512, 768
 WORD_PIECES = ((0, 896), (896, 640), (1536, 384), (1920, 128))
 VECTOR_START = 512
 BACK = 128
@@ -58,13 +59,11 @@ def tile_routed_moe_kernel(tc, xT, w_words, w_scales, b, gate, offs, pos1, pos2,
         nc.vector.memset(ws_sb[:].rearrange("p e n -> p (e n)").bitcast(I32), 0)
 
         x_rows = xT.rearrange("(p j) t -> p j t", j=PACK)
-        raws = []
+        raw = keep.tile([P, PACK, T], F32, name="raw")
+        nc.sync.dma_start(out=raw[:, 0:2, :], in_=x_rows[:, 0:2, :])
         for t0, n in LOADS:
-            raw = stage.tile([P, PACK, n], F32, name="raw", bufs=len(LOADS))
-            nc.sync.dma_start(out=raw[:], in_=x_rows[:, :, t0 : t0 + n])
-            raws.append(raw)
-            if t0 == 896:
-                nc.sync.dma_start(offs_sb[:], offs)
+            nc.sync.dma_start(out=raw[:, 2:4, t0 : t0 + n], in_=x_rows[:, 2:4, t0 : t0 + n])
+        nc.sync.dma_start(offs_sb[:], offs)
         for q in range(4):
             nc.sync.dma_start(
                 out=ws_sb[32 * q : 32 * q + 4, :, :].bitcast(I32),
@@ -76,33 +75,31 @@ def tile_routed_moe_kernel(tc, xT, w_words, w_scales, b, gate, offs, pos1, pos2,
         nc.sync.dma_start(pos2_sb[:], pos2)
         nc.sync.dma_start(out=gates[:], in_=gate.rearrange("g n t -> n g t"))
 
-        def interleave(chunk):
-            load, t0, n, nv = chunk
-            raw, r0 = raws[load], t0 - LOADS[load][0]
-            grouped = stage.tile([P, n, PACK], BF16, name="grouped", bufs=len(CHUNKS), align_bytes=64)
-            nc.vector.tensor_copy(
-                out=grouped[:, 0:nv, :].rearrange("p (c i) j -> p c j i", i=4),
-                in_=raw[:, :, r0 : r0 + nv].rearrange("p j (c i) -> p c j i", i=4),
-            )
-            nc.scalar.copy(
-                out=grouped[:, nv:n, :].rearrange("p (c i) j -> p c j i", i=4),
-                in_=raw[:, :, r0 + nv : r0 + n].rearrange("p j (c i) -> p c j i", i=4),
-            )
-            return grouped
+        grouped = keep.tile([P, T, PACK], BF16, name="grouped", align_bytes=64)
 
-        def quantise(chunk, grouped):
-            load, t0, n, nv = chunk
+        def four_rows(copy, t0, t1):
+            copy(
+                out=grouped[:, t0:t1, :].rearrange("p (c i) j -> p c j i", i=4),
+                in_=raw[:, :, t0:t1].rearrange("p j (c i) -> p c j i", i=4),
+            )
+
+        def two_rows(copy, j0, t0, t1):
+            copy(out=grouped[:, t0:t1, j0 : j0 + 2], in_=raw[:, j0 : j0 + 2, t0:t1].rearrange("p j n -> p n j"))
+
+        two_rows(nc.scalar.copy, 0, EARLY_SCALAR, T)
+        two_rows(nc.vector.tensor_copy, 0, EARLY_VECTOR, EARLY_SCALAR)
+        for t0, n, nv in CHUNKS:
+            if t0 < EARLY_VECTOR:
+                four_rows(nc.vector.tensor_copy, t0, t0 + nv)
+                four_rows(nc.scalar.copy, t0 + nv, t0 + n)
+            else:
+                two_rows(nc.vector.tensor_copy, 2, t0, t0 + nv)
+                two_rows(nc.scalar.copy, 2, t0 + nv, t0 + n)
             nc.vector.quantize_mx(
                 out=x_words[:, t0 : t0 + n].bitcast(FP8X4),
                 scales=x_scales[:, t0 : t0 + n],
-                in_=grouped[:].rearrange("p n j -> p (n j)"),
+                in_=grouped[:, t0 : t0 + n, :].rearrange("p n j -> p (n j)"),
             )
-
-        for load in range(len(LOADS)):
-            chunks = [c for c in CHUNKS if c[0] == load]
-            grouped = [interleave(c) for c in chunks]
-            for c, g in zip(chunks, grouped):
-                quantise(c, g)
 
         nc.vector.tensor_copy(out=s_scales[:], in_=x_scales[:].indirect(offs_sb[:]))
         for j0, n in WORD_PIECES:

@@ -22,9 +22,9 @@ MULT = mybir.AluOpType.mult
 
 FLOPS = 2 * K * N * SLOTS
 
-LOADS = ((0, 256), (256, 256), (512, 256), (768, 128), (896, 128))
-CHUNKS = ((0, 256, 176), (256, 256, 144), (512, 256, 160), (768, 128, 80), (896, 128, 88))
-EARLY_VECTOR, EARLY_SCALAR = 512, 768
+LOADS = ((0, 512), (512, 256), (768, 128), (896, 128))
+CHUNKS = ((0, 256, 192), (256, 256, 96), (512, 256, 96), (768, 128, 48), (896, 128, 88))
+EARLY_VECTOR, EARLY_SCALAR = 0, 688
 WORD_PIECES = ((0, 896), (896, 640), (1536, 384), (1920, 128))
 VECTOR_START = 512
 BACK = 128

@@ -26,9 +26,9 @@ LOADS = ((0, 512), (512, 256), (768, 128), (896, 128))
 CHUNKS = ((0, 256, 192), (256, 256, 96), (512, 256, 96), (768, 128, 48), (896, 128, 88))
 EARLY_VECTOR, EARLY_SCALAR = 0, 688
 WORD_PIECES = ((0, 896), (896, 640), (1536, 384), (1920, 128))
-VECTOR_START = 512
-BACK = 128
-TOKEN_PIECES = ((512, 256), (768, 128), (896, 128))
+VECTOR_START = 384
+BACK = 384
+TOKEN_PIECES = ((384, 320), (704, 192), (896, 128))
 
 
 def tile_routed_moe_kernel(tc, xT, w_words, w_scales, b, gate, offs, pos1, pos2, out):

@@ -7,6 +7,7 @@ K, T, E, C, N = 512, 1024, 8, 256, 128
 SLOTS = E * C
 P = 128
 PACK = 4
+LIST = 16
 
 F32 = mybir.dt.float32
 BF16 = mybir.dt.bfloat16
@@ -22,13 +23,14 @@ MULT = mybir.AluOpType.mult
 
 FLOPS = 2 * K * N * SLOTS
 
-LOADS = ((0, 512), (512, 256), (768, 128), (896, 128))
-CHUNKS = ((0, 256, 192), (256, 256, 96), (512, 256, 96), (768, 128, 48), (896, 128, 88))
-EARLY_VECTOR, EARLY_SCALAR = 0, 688
+LATE_LOADS = ((0, 512), (512, 256), (768, 128), (896, 128))
+EARLY_CUT = 688
+QUANTISE_PIECES = ((0, 256, True, 192), (256, 256, True, 96), (512, 256, True, 112), (768, 256, False, 128))
 WORD_PIECES = ((0, 896), (896, 640), (1536, 384), (1920, 128))
-VECTOR_START = 384
-BACK = 384
-TOKEN_PIECES = ((384, 320), (704, 192), (896, 128))
+NARROW_MOST = 3 * T // 4
+TENSOR_TOKENS = 512
+STORE_TOKENS = 256
+VECTOR_PIECES = ((512, 320), (832, 192))
 
 
 def tile_routed_moe_kernel(tc, xT, w_words, w_scales, b, gate, offs, pos1, pos2, out):
@@ -38,11 +40,11 @@ def tile_routed_moe_kernel(tc, xT, w_words, w_scales, b, gate, offs, pos1, pos2,
         stage = ctx.enter_context(tc.tile_pool(name="stage", bufs=4))
         psum = ctx.enter_context(tc.psum_pool(name="psum", bufs=8))
 
-        offs_sb = keep.tile([P, SLOTS // 16], U16, name="offs_sb")
-        pos1_sb = keep.tile([P, T // 16], U16, name="pos1_sb")
-        pos2_sb = keep.tile([P, T // 16], U16, name="pos2_sb")
+        offs_sb = keep.tile([P, SLOTS // LIST], U16, name="offs_sb")
+        pos1_sb = keep.tile([P, T // LIST], U16, name="pos1_sb")
+        pos2_sb = keep.tile([P, T // LIST], U16, name="pos2_sb")
         x_words = keep.tile([P, 2 * T], U32, name="x_words", align_bytes=64)
-        x_scales = keep.tile([P, 4 * T], U8, name="x_scales", align_bytes=64)
+        x_scales = keep.tile([P, 2 * SLOTS], U8, name="x_scales", align_bytes=64)
         s_words = keep.tile([P, SLOTS], U32, name="s_words", align_bytes=64)
         s_scales = keep.tile([P, SLOTS], U8, name="s_scales", align_bytes=64)
         w_sb = keep.tile([P, E, N * PACK], U8, name="w_sb", align_bytes=64)
@@ -61,13 +63,13 @@ def tile_routed_moe_kernel(tc, xT, w_words, w_scales, b, gate, offs, pos1, pos2,
         x_rows = xT.rearrange("(p j) t -> p j t", j=PACK)
         raw = keep.tile([P, PACK, T], F32, name="raw")
         nc.sync.dma_start(out=raw[:, 0:2, :], in_=x_rows[:, 0:2, :])
-        for t0, n in LOADS:
+        for t0, n in LATE_LOADS:
             nc.sync.dma_start(out=raw[:, 2:4, t0 : t0 + n], in_=x_rows[:, 2:4, t0 : t0 + n])
         nc.sync.dma_start(offs_sb[:], offs)
-        for q in range(4):
+        for g in range(4):
             nc.sync.dma_start(
-                out=ws_sb[32 * q : 32 * q + 4, :, :].bitcast(I32),
-                in_=w_scales[:, 0, 4 * q : 4 * q + 4, :].rearrange("e q n -> q e n").bitcast(I32),
+                out=ws_sb[32 * g : 32 * g + 4, :, :].bitcast(I32),
+                in_=w_scales[:, 0, 4 * g : 4 * g + 4, :].rearrange("e q n -> q e n").bitcast(I32),
             )
         nc.sync.dma_start(out=w_sb[:], in_=w_words.rearrange("e a p n r -> p (e a) (n r)"))
         nc.sync.dma_start(out=b_sb[:], in_=b)
@@ -77,34 +79,33 @@ def tile_routed_moe_kernel(tc, xT, w_words, w_scales, b, gate, offs, pos1, pos2,
 
         grouped = keep.tile([P, T, PACK], BF16, name="grouped", align_bytes=64)
 
-        def four_rows(copy, t0, t1):
-            copy(
-                out=grouped[:, t0:t1, :].rearrange("p (c i) j -> p c j i", i=4),
-                in_=raw[:, :, t0:t1].rearrange("p j (c i) -> p c j i", i=4),
-            )
-
         def two_rows(copy, j0, t0, t1):
             copy(out=grouped[:, t0:t1, j0 : j0 + 2], in_=raw[:, j0 : j0 + 2, t0:t1].rearrange("p j n -> p n j"))
 
-        two_rows(nc.scalar.copy, 0, EARLY_SCALAR, T)
-        two_rows(nc.vector.tensor_copy, 0, EARLY_VECTOR, EARLY_SCALAR)
-        for t0, n, nv in CHUNKS:
-            if t0 < EARLY_VECTOR:
-                four_rows(nc.vector.tensor_copy, t0, t0 + nv)
-                four_rows(nc.scalar.copy, t0 + nv, t0 + n)
-            else:
-                two_rows(nc.vector.tensor_copy, 2, t0, t0 + nv)
-                two_rows(nc.scalar.copy, 2, t0 + nv, t0 + n)
+        def quantise(t0, n):
             nc.vector.quantize_mx(
                 out=x_words[:, t0 : t0 + n].bitcast(FP8X4),
                 scales=x_scales[:, t0 : t0 + n],
                 in_=grouped[:, t0 : t0 + n, :].rearrange("p n j -> p (n j)"),
             )
 
+        two_rows(nc.scalar.copy, 0, EARLY_CUT, T)
+        two_rows(nc.vector.tensor_copy, 0, 0, EARLY_CUT)
+        to_quantise = None
+        for t0, n, vector_first, cut in QUANTISE_PIECES:
+            lower, upper = (nc.vector.tensor_copy, nc.scalar.copy) if vector_first else (nc.scalar.copy, nc.vector.tensor_copy)
+            two_rows(lower, 2, t0, t0 + cut)
+            two_rows(upper, 2, t0 + cut, t0 + n)
+            if to_quantise is not None:
+                quantise(*to_quantise)
+            to_quantise = (t0, n)
+        quantise(*to_quantise)
+
         nc.vector.tensor_copy(out=s_scales[:], in_=x_scales[:].indirect(offs_sb[:]))
+        last_piece_start = WORD_PIECES[-1][0]
         for j0, n in WORD_PIECES:
-            window = x_words[:] if n > 768 else x_words[:, 0:T]
-            nc.vector.tensor_copy(out=s_words[:, j0 : j0 + n], in_=window.indirect(offs_sb[:, j0 // 16 : (j0 + n) // 16]))
+            window = x_words[:] if n > NARROW_MOST else x_words[:, 0:T]
+            nc.vector.tensor_copy(out=s_words[:, j0 : j0 + n], in_=window.indirect(offs_sb[:, j0 // LIST : (j0 + n) // LIST]))
             for e in range(j0 // C, (j0 + n - 1) // C + 1):
                 lo, hi = max(j0, e * C), min(j0 + n, (e + 1) * C)
                 acc = psum.tile([N, hi - lo], F32, name="bank")
@@ -117,54 +118,49 @@ def tile_routed_moe_kernel(tc, xT, w_words, w_scales, b, gate, offs, pos1, pos2,
                     start=True,
                     stop=True,
                 )
-                if hi == WORD_PIECES[-1][0]:
+                if hi == last_piece_start:
                     nc.vector.tensor_scalar(y[:, lo:hi], acc[:], b_sb[:, e : e + 1], 0.0, ADD, MAX)
                 else:
                     nc.scalar.activation(y[:, lo:hi], acc[:], RELU, bias=b_sb[:, e : e + 1])
 
-        def gated(pos_sb, gate_sb, t0, n, name):
-            part = keep.tile([P, n], F32, name=name)
-            nc.vector.tensor_tensor(part[:], y[:].indirect(pos_sb[:, t0 // 16 : (t0 + n) // 16]), gate_sb[:, t0 : t0 + n], MULT)
+        def gated(pool, pos_sb, gate_sb, t0, n, name):
+            part = pool.tile([P, n], F32, name=name)
+            nc.vector.tensor_tensor(
+                part[:], y[:].indirect(pos_sb[:, t0 // LIST : (t0 + n) // LIST]), gate_sb[:, t0 : t0 + n], MULT
+            )
             return part
 
-        blocks = range(0, VECTOR_START, P)
-        first = gated(pos1_sb, gate1_sb, 0, VECTOR_START, "first")
+        blocks = range(0, TENSOR_TOKENS, P)
+        first = gated(keep, pos1_sb, gate1_sb, 0, TENSOR_TOKENS, "first")
         turned = [psum.tile([P, P], F32, name="bank") for c0 in blocks]
         for c0, bank in zip(blocks, turned):
             nc.tensor.matmul(bank[:], first[:, c0 : c0 + P], ident[:], start=True, stop=False, is_transpose=True)
-        second = gated(pos2_sb, gate2_sb, 0, VECTOR_START, "second")
+        second = gated(keep, pos2_sb, gate2_sb, 0, TENSOR_TOKENS, "second")
         turned_sb = []
         for c0, bank in zip(blocks, turned):
             nc.tensor.matmul(bank[:], second[:, c0 : c0 + P], ident[:], start=False, stop=True, is_transpose=True)
             held = stage.tile([P, P], F32, name="held", bufs=len(blocks))
             nc.scalar.copy(out=held[:], in_=bank[:])
             turned_sb.append(held)
-        for t0 in range(0, VECTOR_START, BACK):
-            back = psum.tile([P, BACK], F32, name="bank")
-            for c0 in range(0, BACK, P):
+        for t0 in range(0, TENSOR_TOKENS, STORE_TOKENS):
+            back = psum.tile([P, STORE_TOKENS], F32, name="bank")
+            for c0 in range(0, STORE_TOKENS, P):
                 nc.tensor.transpose(back[:, c0 : c0 + P], turned_sb[(t0 + c0) // P][:], ident[:])
-            summed = stage.tile([P, BACK], F32, name="summed", bufs=4)
+            summed = stage.tile([P, STORE_TOKENS], F32, name="summed")
             nc.scalar.copy(out=summed[:], in_=back[:])
-            nc.scalar.dma_start(out=out[:, t0 : t0 + BACK], in_=summed[:])
+            nc.scalar.dma_start(out=out[:, t0 : t0 + STORE_TOKENS], in_=summed[:])
 
-        part1 = gated(pos1_sb, gate1_sb, VECTOR_START, T - VECTOR_START, "part1")
-
-        def second_part(t0, n):
-            part2 = stage.tile([P, n], F32, name="part2")
-            nc.vector.tensor_tensor(
-                part2[:], y[:].indirect(pos2_sb[:, t0 // 16 : (t0 + n) // 16]), gate2_sb[:, t0 : t0 + n], MULT
-            )
-            return part2
+        part1 = gated(keep, pos1_sb, gate1_sb, TENSOR_TOKENS, T - TENSOR_TOKENS, "part1")
 
         def add_and_store(t0, n, part2):
             total = stage.tile([P, n], F32, name="total")
-            nc.vector.tensor_tensor(total[:], part1[:, t0 - VECTOR_START : t0 - VECTOR_START + n], part2[:], ADD)
+            nc.vector.tensor_tensor(total[:], part1[:, t0 - TENSOR_TOKENS : t0 - TENSOR_TOKENS + n], part2[:], ADD)
             nc.sync.dma_start(out=out[:, t0 : t0 + n], in_=total[:])
 
-        waiting = None
-        for t0, n in TOKEN_PIECES:
-            part2 = second_part(t0, n)
-            if waiting is not None:
-                add_and_store(*waiting)
-            waiting = (t0, n, part2)
-        add_and_store(*waiting)
+        to_add = None
+        for t0, n in VECTOR_PIECES:
+            part2 = gated(stage, pos2_sb, gate2_sb, t0, n, "part2")
+            if to_add is not None:
+                add_and_store(*to_add)
+            to_add = (t0, n, part2)
+        add_and_store(*to_add)

@@ -16,6 +16,7 @@ I32 = mybir.dt.int32
 U16 = mybir.dt.uint16
 U8 = mybir.dt.uint8
 FP8X4 = mybir.dt.float8_e4m3fn_x4
+COPY = mybir.ActivationFunctionType.Copy
 RELU = mybir.ActivationFunctionType.Relu
 ADD = mybir.AluOpType.add
 MAX = mybir.AluOpType.max
@@ -23,11 +24,13 @@ MULT = mybir.AluOpType.mult
 
 FLOPS = 2 * K * N * SLOTS
 
-LATE_LOADS = ((0, 512), (512, 256), (768, 128), (896, 128))
-EARLY_CUT = 688
-QUANTISE_PIECES = ((0, 256, True, 192), (256, 256, True, 96), (512, 256, True, 112), (768, 256, False, 128))
-WORD_PIECES = ((0, 896), (896, 640), (1536, 384), (1920, 128))
-NARROW_MOST = 3 * T // 4
+
+ROW2_CUT = 688
+PAIR_LOADS = ((0, 512), (512, 512))
+LOW_PIECES = ((0, 512), (512, 1536))
+ROW2_PIECES = ((0, 1024), (1024, 1024))
+SLOT_PIECES = ((0, 512), (512, 512), (1024, 512), (1536, 256), (1792, 128), (1920, 128))
+
 TENSOR_TOKENS = 512
 STORE_TOKENS = 256
 VECTOR_PIECES = ((512, 320), (832, 192))
@@ -43,8 +46,12 @@ def tile_routed_moe_kernel(tc, xT, w_words, w_scales, b, gate, offs, pos1, pos2,
         offs_sb = keep.tile([P, SLOTS // LIST], U16, name="offs_sb")
         pos1_sb = keep.tile([P, T // LIST], U16, name="pos1_sb")
         pos2_sb = keep.tile([P, T // LIST], U16, name="pos2_sb")
-        x_words = keep.tile([P, 2 * T], U32, name="x_words", align_bytes=64)
-        x_scales = keep.tile([P, 2 * SLOTS], U8, name="x_scales", align_bytes=64)
+        raw = keep.tile([P, PACK - 1, T], F32, name="raw")
+        low = keep.tile([P, 2 * T], U32, name="low", align_bytes=64)
+        row2 = keep.tile([P, 2 * T], BF16, name="row2", align_bytes=64)
+        row3 = keep.tile([P, T], BF16, name="row3", align_bytes=64)
+        pairs = keep.tile([P, 2, SLOTS], U32, name="pairs", align_bytes=64)
+        grouped = keep.tile([P, SLOTS * PACK], BF16, name="grouped", align_bytes=64)
         s_words = keep.tile([P, SLOTS], U32, name="s_words", align_bytes=64)
         s_scales = keep.tile([P, SLOTS], U8, name="s_scales", align_bytes=64)
         w_sb = keep.tile([P, E, N * PACK], U8, name="w_sb", align_bytes=64)
@@ -56,16 +63,17 @@ def tile_routed_moe_kernel(tc, xT, w_words, w_scales, b, gate, offs, pos1, pos2,
         ident = keep.tile([P, P], F32, name="ident")
         make_identity(nc, ident[:])
 
-        nc.vector.memset(x_scales[:].bitcast(I32), 0)
-        nc.vector.memset(x_words[:, T : 2 * T].bitcast(I32), 0)
+        nc.vector.memset(row2[:, T : 2 * T].bitcast(I32), 0)
+        nc.vector.memset(low[:, T : 2 * T].bitcast(I32), 0)
         nc.vector.memset(ws_sb[:].rearrange("p e n -> p (e n)").bitcast(I32), 0)
 
         x_rows = xT.rearrange("(p j) t -> p j t", j=PACK)
-        raw = keep.tile([P, PACK, T], F32, name="raw")
-        nc.sync.dma_start(out=raw[:, 0:2, :], in_=x_rows[:, 0:2, :])
-        for t0, n in LATE_LOADS:
-            nc.sync.dma_start(out=raw[:, 2:4, t0 : t0 + n], in_=x_rows[:, 2:4, t0 : t0 + n])
+        nc.sync.dma_start(out=raw[:, 2, :], in_=x_rows[:, 2, :])
         nc.sync.dma_start(offs_sb[:], offs)
+        for t0, n in PAIR_LOADS:
+            nc.sync.dma_start(out=raw[:, 0:2, t0 : t0 + n], in_=x_rows[:, 0:2, t0 : t0 + n])
+        raw3 = pairs[:, 0, SLOTS - T : SLOTS].bitcast(F32)
+        nc.sync.dma_start(out=raw3, in_=x_rows[:, 3, :])
         for g in range(4):
             nc.sync.dma_start(
                 out=ws_sb[32 * g : 32 * g + 4, :, :].bitcast(I32),
@@ -77,35 +85,39 @@ def tile_routed_moe_kernel(tc, xT, w_words, w_scales, b, gate, offs, pos1, pos2,
         nc.sync.dma_start(pos2_sb[:], pos2)
         nc.sync.dma_start(out=gates[:], in_=gate.rearrange("g n t -> n g t"))
 
-        grouped = keep.tile([P, T, PACK], BF16, name="grouped", align_bytes=64)
+        def slots_of(j0, n):
+            return offs_sb[:, j0 // LIST : (j0 + n) // LIST]
 
-        def two_rows(copy, j0, t0, t1):
-            copy(out=grouped[:, t0:t1, j0 : j0 + 2], in_=raw[:, j0 : j0 + 2, t0:t1].rearrange("p j n -> p n j"))
+        high = pairs[:, 1, :].bitcast(BF16).rearrange("p (n e) -> p n e", e=2)
 
-        def quantise(t0, n):
-            nc.vector.quantize_mx(
-                out=x_words[:, t0 : t0 + n].bitcast(FP8X4),
-                scales=x_scales[:, t0 : t0 + n],
-                in_=grouped[:, t0 : t0 + n, :].rearrange("p n j -> p (n j)"),
+        nc.scalar.copy(out=row2[:, ROW2_CUT:T], in_=raw[:, 2, ROW2_CUT:T])
+        nc.vector.tensor_copy(out=row2[:, 0:ROW2_CUT], in_=raw[:, 2, 0:ROW2_CUT])
+        for j0, n in ROW2_PIECES:
+            nc.scalar.activation(high[:, j0 : j0 + n, 0], row2[:].indirect(slots_of(j0, n)), COPY)
+        for t0, n in PAIR_LOADS:
+            nc.vector.tensor_copy(
+                out=low[:, t0 : t0 + n].bitcast(BF16).rearrange("p (n j) -> p n j", j=2),
+                in_=raw[:, 0:2, t0 : t0 + n].rearrange("p j n -> p n j"),
+            )
+        for i, (j0, n) in enumerate(LOW_PIECES):
+            nc.vector.tensor_copy(out=pairs[:, 0, j0 : j0 + n], in_=low[:].indirect(slots_of(j0, n)))
+            if i == 0:
+                nc.vector.tensor_copy(out=row3[:], in_=raw3)
+        for j0, n in SLOT_PIECES:
+            nc.scalar.activation(high[:, j0 : j0 + n, 1], row3[:].indirect(slots_of(j0, n)), COPY)
+
+        def side_by_side(j0, n):
+            nc.vector.tensor_copy(
+                out=grouped[:, PACK * j0 : PACK * (j0 + n)].bitcast(F32).rearrange("p (n u) -> p n u", u=2),
+                in_=pairs[:, :, j0 : j0 + n].bitcast(F32).rearrange("p u n -> p n u"),
             )
 
-        two_rows(nc.scalar.copy, 0, EARLY_CUT, T)
-        two_rows(nc.vector.tensor_copy, 0, 0, EARLY_CUT)
-        to_quantise = None
-        for t0, n, vector_first, cut in QUANTISE_PIECES:
-            lower, upper = (nc.vector.tensor_copy, nc.scalar.copy) if vector_first else (nc.scalar.copy, nc.vector.tensor_copy)
-            two_rows(lower, 2, t0, t0 + cut)
-            two_rows(upper, 2, t0 + cut, t0 + n)
-            if to_quantise is not None:
-                quantise(*to_quantise)
-            to_quantise = (t0, n)
-        quantise(*to_quantise)
-
-        nc.vector.tensor_copy(out=s_scales[:], in_=x_scales[:].indirect(offs_sb[:]))
-        last_piece_start = WORD_PIECES[-1][0]
-        for j0, n in WORD_PIECES:
-            window = x_words[:] if n > NARROW_MOST else x_words[:, 0:T]
-            nc.vector.tensor_copy(out=s_words[:, j0 : j0 + n], in_=window.indirect(offs_sb[:, j0 // LIST : (j0 + n) // LIST]))
+        def quantise_and_multiply(j0, n):
+            nc.vector.quantize_mx(
+                out=s_words[:, j0 : j0 + n].bitcast(FP8X4),
+                scales=s_scales[:, j0 : j0 + n],
+                in_=grouped[:, PACK * j0 : PACK * (j0 + n)],
+            )
             for e in range(j0 // C, (j0 + n - 1) // C + 1):
                 lo, hi = max(j0, e * C), min(j0 + n, (e + 1) * C)
                 acc = psum.tile([N, hi - lo], F32, name="bank")
@@ -118,10 +130,18 @@ def tile_routed_moe_kernel(tc, xT, w_words, w_scales, b, gate, offs, pos1, pos2,
                     start=True,
                     stop=True,
                 )
-                if hi == last_piece_start:
+                if hi == SLOT_PIECES[-1][0]:
                     nc.vector.tensor_scalar(y[:, lo:hi], acc[:], b_sb[:, e : e + 1], 0.0, ADD, MAX)
                 else:
                     nc.scalar.activation(y[:, lo:hi], acc[:], RELU, bias=b_sb[:, e : e + 1])
+
+        waiting = None
+        for piece in SLOT_PIECES:
+            side_by_side(*piece)
+            if waiting is not None:
+                quantise_and_multiply(*waiting)
+            waiting = piece
+        quantise_and_multiply(*waiting)
 
         def gated(pool, pos_sb, gate_sb, t0, n, name):
             part = pool.tile([P, n], F32, name=name)

@@ -25,11 +25,11 @@ MULT = mybir.AluOpType.mult
 FLOPS = 2 * K * N * SLOTS
 
 
+PIECE = 512
+PIECES = SLOTS // PIECE
 ROW2_CUT = 688
-PAIR_LOADS = ((0, 512), (512, 512))
-LOW_PIECES = ((0, 512), (512, 1536))
-ROW2_PIECES = ((0, 1024), (1024, 1024))
-SLOT_PIECES = ((0, 512), (512, 512), (1024, 512), (1536, 256), (1792, 128), (1920, 128))
+PAIR_LOADS = ((0, 640), (640, 384))
+VECTOR_EMPTIES = (1536, 1792)
 
 TENSOR_TOKENS = 512
 STORE_TOKENS = 256
@@ -41,17 +41,20 @@ def tile_routed_moe_kernel(tc, xT, w_words, w_scales, b, gate, offs, pos1, pos2,
     with ExitStack() as ctx:
         keep = ctx.enter_context(tc.tile_pool(name="keep", bufs=1))
         stage = ctx.enter_context(tc.tile_pool(name="stage", bufs=4))
+        turns = ctx.enter_context(tc.tile_pool(name="turns", bufs=1))
         psum = ctx.enter_context(tc.psum_pool(name="psum", bufs=8))
 
         offs_sb = keep.tile([P, SLOTS // LIST], U16, name="offs_sb")
         pos1_sb = keep.tile([P, T // LIST], U16, name="pos1_sb")
         pos2_sb = keep.tile([P, T // LIST], U16, name="pos2_sb")
         raw = keep.tile([P, PACK - 1, T], F32, name="raw")
-        low = keep.tile([P, 2 * T], U32, name="low", align_bytes=64)
+        low = keep.tile([P, T], U32, name="low", align_bytes=64)
         row2 = keep.tile([P, 2 * T], BF16, name="row2", align_bytes=64)
-        row3 = keep.tile([P, T], BF16, name="row3", align_bytes=64)
-        pairs = keep.tile([P, 2, SLOTS], U32, name="pairs", align_bytes=64)
-        grouped = keep.tile([P, SLOTS * PACK], BF16, name="grouped", align_bytes=64)
+        row3 = keep.tile([P, 2 * T], BF16, name="row3", align_bytes=64)
+        early = keep.tile([P, 2, 2, PIECE], U32, name="early", align_bytes=64)
+        late = turns.tile([P, 2, 2, PIECE], U32, name="late", tag="turns", align_bytes=64)
+        pairs = [early[:, 0, :, :], early[:, 1, :, :], late[:, 0, :, :], late[:, 1, :, :]]
+        fresh = keep.tile([P, 2, 2 * PIECE], U32, name="fresh", align_bytes=64)
         s_words = keep.tile([P, SLOTS], U32, name="s_words", align_bytes=64)
         s_scales = keep.tile([P, SLOTS], U8, name="s_scales", align_bytes=64)
         w_sb = keep.tile([P, E, N * PACK], U8, name="w_sb", align_bytes=64)
@@ -59,21 +62,20 @@ def tile_routed_moe_kernel(tc, xT, w_words, w_scales, b, gate, offs, pos1, pos2,
         b_sb = keep.tile([P, E], F32, name="b_sb")
         gates = keep.tile([P, 2, T], F32, name="gates")
         gate1_sb, gate2_sb = gates[:, 0, :], gates[:, 1, :]
-        y = keep.tile([P, SLOTS], F32, name="y")
         ident = keep.tile([P, P], F32, name="ident")
         make_identity(nc, ident[:])
 
         nc.vector.memset(row2[:, T : 2 * T].bitcast(I32), 0)
-        nc.vector.memset(low[:, T : 2 * T].bitcast(I32), 0)
+        nc.vector.memset(row3[:, T : 2 * T].bitcast(I32), 0)
         nc.vector.memset(ws_sb[:].rearrange("p e n -> p (e n)").bitcast(I32), 0)
 
         x_rows = xT.rearrange("(p j) t -> p j t", j=PACK)
         nc.sync.dma_start(out=raw[:, 2, :], in_=x_rows[:, 2, :])
         nc.sync.dma_start(offs_sb[:], offs)
+        raw3 = late[:].rearrange("p i u n -> p (i u n)")[:, PIECE : 3 * PIECE].bitcast(F32)
+        nc.sync.dma_start(out=raw3, in_=x_rows[:, 3, :])
         for t0, n in PAIR_LOADS:
             nc.sync.dma_start(out=raw[:, 0:2, t0 : t0 + n], in_=x_rows[:, 0:2, t0 : t0 + n])
-        raw3 = pairs[:, 0, SLOTS - T : SLOTS].bitcast(F32)
-        nc.sync.dma_start(out=raw3, in_=x_rows[:, 3, :])
         for g in range(4):
             nc.sync.dma_start(
                 out=ws_sb[32 * g : 32 * g + 4, :, :].bitcast(I32),
@@ -88,35 +90,27 @@ def tile_routed_moe_kernel(tc, xT, w_words, w_scales, b, gate, offs, pos1, pos2,
         def slots_of(j0, n):
             return offs_sb[:, j0 // LIST : (j0 + n) // LIST]
 
-        high = pairs[:, 1, :].bitcast(BF16).rearrange("p (n e) -> p n e", e=2)
+        high_early = early[:, :, 1, :].bitcast(BF16).rearrange("p i (n e) -> p i n e", e=2)
+        high_late = late[:, :, 1, :].bitcast(BF16).rearrange("p i (n e) -> p i n e", e=2)
+        grouped = [fresh[:, 0, :], fresh[:, 1, :]] + [pairs[i].rearrange("p u n -> p (u n)") for i in range(2)]
 
-        nc.scalar.copy(out=row2[:, ROW2_CUT:T], in_=raw[:, 2, ROW2_CUT:T])
-        nc.vector.tensor_copy(out=row2[:, 0:ROW2_CUT], in_=raw[:, 2, 0:ROW2_CUT])
-        for j0, n in ROW2_PIECES:
-            nc.scalar.activation(high[:, j0 : j0 + n, 0], row2[:].indirect(slots_of(j0, n)), COPY)
-        for t0, n in PAIR_LOADS:
+        def round_pairs(t0, n):
             nc.vector.tensor_copy(
                 out=low[:, t0 : t0 + n].bitcast(BF16).rearrange("p (n j) -> p n j", j=2),
                 in_=raw[:, 0:2, t0 : t0 + n].rearrange("p j n -> p n j"),
             )
-        for i, (j0, n) in enumerate(LOW_PIECES):
-            nc.vector.tensor_copy(out=pairs[:, 0, j0 : j0 + n], in_=low[:].indirect(slots_of(j0, n)))
-            if i == 0:
-                nc.vector.tensor_copy(out=row3[:], in_=raw3)
-        for j0, n in SLOT_PIECES:
-            nc.scalar.activation(high[:, j0 : j0 + n, 1], row3[:].indirect(slots_of(j0, n)), COPY)
 
-        def side_by_side(j0, n):
-            nc.vector.tensor_copy(
-                out=grouped[:, PACK * j0 : PACK * (j0 + n)].bitcast(F32).rearrange("p (n u) -> p n u", u=2),
-                in_=pairs[:, :, j0 : j0 + n].bitcast(F32).rearrange("p u n -> p n u"),
+        def side_by_side(copy, dtype, i, c0, n):
+            copy(
+                out=grouped[i][:, 2 * c0 : 2 * (c0 + n)].bitcast(dtype).rearrange("p (n u) -> p n u", u=2),
+                in_=pairs[i][:, :, c0 : c0 + n].bitcast(dtype).rearrange("p u n -> p n u"),
             )
 
         def quantise_and_multiply(j0, n):
             nc.vector.quantize_mx(
                 out=s_words[:, j0 : j0 + n].bitcast(FP8X4),
                 scales=s_scales[:, j0 : j0 + n],
-                in_=grouped[:, PACK * j0 : PACK * (j0 + n)],
+                in_=grouped[j0 // PIECE][:, 2 * (j0 % PIECE) : 2 * (j0 % PIECE + n)].bitcast(BF16),
             )
             for e in range(j0 // C, (j0 + n - 1) // C + 1):
                 lo, hi = max(j0, e * C), min(j0 + n, (e + 1) * C)
@@ -130,18 +124,35 @@ def tile_routed_moe_kernel(tc, xT, w_words, w_scales, b, gate, offs, pos1, pos2,
                     start=True,
                     stop=True,
                 )
-                if hi == SLOT_PIECES[-1][0]:
+                if lo in VECTOR_EMPTIES:
                     nc.vector.tensor_scalar(y[:, lo:hi], acc[:], b_sb[:, e : e + 1], 0.0, ADD, MAX)
                 else:
                     nc.scalar.activation(y[:, lo:hi], acc[:], RELU, bias=b_sb[:, e : e + 1])
 
-        waiting = None
-        for piece in SLOT_PIECES:
-            side_by_side(*piece)
-            if waiting is not None:
-                quantise_and_multiply(*waiting)
-            waiting = piece
-        quantise_and_multiply(*waiting)
+        nc.scalar.copy(out=row2[:, ROW2_CUT:T], in_=raw[:, 2, ROW2_CUT:T])
+        nc.vector.tensor_copy(out=row2[:, 0:ROW2_CUT], in_=raw[:, 2, 0:ROW2_CUT])
+        nc.gpsimd.tensor_copy(out=row3[:, 0:T], in_=raw3)
+        for row, window in ((0, raw[:, 2, :]), (1, raw3)):
+            nc.vector.tensor_copy(out=high_late[:, 1, :, row], in_=window.indirect(slots_of(3 * PIECE, PIECE)))
+        for row, window in ((0, row2), (1, row3)):
+            nc.scalar.activation(high_early[:, :, :, row], window[:].indirect(slots_of(0, 2 * PIECE)), COPY)
+        for row, window in ((0, row2), (1, row3)):
+            nc.scalar.activation(high_late[:, 0, :, row], window[:].indirect(slots_of(2 * PIECE, PIECE)), COPY)
+        for t0, n in PAIR_LOADS:
+            round_pairs(t0, n)
+        for i in range(PIECES):
+            nc.vector.tensor_copy(out=pairs[i][:, 0, :], in_=low[:, 0:T].indirect(slots_of(i * PIECE, PIECE)))
+        for i in range(2):
+            side_by_side(nc.gpsimd.tensor_copy, U32, i, 0, PIECE)
+        for i in range(2, 4):
+            side_by_side(nc.scalar.copy, U32, i, 0, PIECE)
+        y = turns.tile([P, SLOTS], F32, name="y", tag="turns", align_bytes=64)
+        quantise_and_multiply(0, 512)
+        quantise_and_multiply(512, 512)
+        quantise_and_multiply(1024, 512)
+        quantise_and_multiply(1536, 256)
+        quantise_and_multiply(1792, 128)
+        quantise_and_multiply(1920, 128)
 
         def gated(pool, pos_sb, gate_sb, t0, n, name):
             part = pool.tile([P, n], F32, name=name)

@@ -29,7 +29,7 @@ PIECE = 512
 PIECES = SLOTS // PIECE
 ROW2_CUT = 688
 PAIR_LOADS = ((0, 640), (640, 384))
-VECTOR_EMPTIES = (1536, 1792)
+VECTOR_EMPTIES = (768, 1536)
 
 TENSOR_TOKENS = 512
 STORE_TOKENS = 256
@@ -106,6 +106,8 @@ def tile_routed_moe_kernel(tc, xT, w_words, w_scales, b, gate, offs, pos1, pos2,
                 in_=pairs[i][:, :, c0 : c0 + n].bitcast(dtype).rearrange("p u n -> p n u"),
             )
 
+        for_vector = []
+
         def quantise_and_multiply(j0, n):
             nc.vector.quantize_mx(
                 out=s_words[:, j0 : j0 + n].bitcast(FP8X4),
@@ -125,7 +127,7 @@ def tile_routed_moe_kernel(tc, xT, w_words, w_scales, b, gate, offs, pos1, pos2,
                     stop=True,
                 )
                 if lo in VECTOR_EMPTIES:
-                    nc.vector.tensor_scalar(y[:, lo:hi], acc[:], b_sb[:, e : e + 1], 0.0, ADD, MAX)
+                    for_vector.append((lo, hi, acc, e))
                 else:
                     nc.scalar.activation(y[:, lo:hi], acc[:], RELU, bias=b_sb[:, e : e + 1])
 
@@ -153,6 +155,8 @@ def tile_routed_moe_kernel(tc, xT, w_words, w_scales, b, gate, offs, pos1, pos2,
         quantise_and_multiply(1536, 256)
         quantise_and_multiply(1792, 128)
         quantise_and_multiply(1920, 128)
+        for lo, hi, acc, e in for_vector:
+            nc.vector.tensor_scalar(y[:, lo:hi], acc[:], b_sb[:, e : e + 1], 0.0, ADD, MAX)
 
         def gated(pool, pos_sb, gate_sb, t0, n, name):
             part = pool.tile([P, n], F32, name=name)

@@ -144,8 +144,9 @@ def tile_routed_moe_kernel(tc, xT, w_words, w_scales, b, gate, offs, pos1, pos2,
             round_pairs(t0, n)
         for i in range(PIECES):
             nc.vector.tensor_copy(out=pairs[i][:, 0, :], in_=low[:, 0:T].indirect(slots_of(i * PIECE, PIECE)))
-        for i in range(2):
-            side_by_side(nc.gpsimd.tensor_copy, U32, i, 0, PIECE)
+        side_by_side(nc.gpsimd.tensor_copy, U32, 0, 0, PIECE)
+        side_by_side(nc.gpsimd.tensor_copy, U32, 1, 0, 384)
+        side_by_side(nc.scalar.copy, U32, 1, 384, 128)
         for i in range(2, 4):
             side_by_side(nc.scalar.copy, U32, i, 0, PIECE)
         y = turns.tile([P, SLOTS], F32, name="y", tag="turns", align_bytes=64)

@@ -28,7 +28,7 @@ FLOPS = 2 * K * N * SLOTS
 PIECE = 512
 PIECES = SLOTS // PIECE
 ROW2_CUT = 688
-PAIR_LOADS = ((0, 640), (640, 384))
+PAIR_LOADS = ((0, 576), (576, 448))
 VECTOR_EMPTIES = (768, 1536)
 
 TENSOR_TOKENS = 512
@@ -74,8 +74,11 @@ def tile_routed_moe_kernel(tc, xT, w_words, w_scales, b, gate, offs, pos1, pos2,
         nc.sync.dma_start(offs_sb[:], offs)
         raw3 = late[:].rearrange("p i u n -> p (i u n)")[:, PIECE : 3 * PIECE].bitcast(F32)
         nc.sync.dma_start(out=raw3, in_=x_rows[:, 3, :])
-        for t0, n in PAIR_LOADS:
-            nc.sync.dma_start(out=raw[:, 0:2, t0 : t0 + n], in_=x_rows[:, 0:2, t0 : t0 + n])
+        raw_flat = raw[:].rearrange("p j t -> p (j t)")
+        x_flat = xT.rearrange("(p j) t -> p (j t)", j=PACK)
+        cut = T + PAIR_LOADS[1][0]
+        nc.sync.dma_start(out=raw_flat[:, 0:cut], in_=x_flat[:, 0:cut])
+        nc.sync.dma_start(out=raw_flat[:, cut : 2 * T], in_=x_flat[:, cut : 2 * T])
         for g in range(4):
             nc.sync.dma_start(
                 out=ws_sb[32 * g : 32 * g + 4, :, :].bitcast(I32),

@@ -24,13 +24,12 @@ MULT = mybir.AluOpType.mult
 
 FLOPS = 2 * K * N * SLOTS
 
-
 PIECE = 512
 PIECES = SLOTS // PIECE
 ROW2_CUT = 688
-PAIR_LOADS = ((0, 576), (576, 448))
-VECTOR_EMPTIES = (768, 1536)
-
+ROW1_PIECES = ((0, 384), (384, 384), (768, 256))
+QUANTISE_PIECES = ((0, 512), (512, 512), (1024, 512), (1536, 256), (1792, 128), (1920, 128))
+VECTOR_EMPTIES = (3, 6)
 TENSOR_TOKENS = 512
 STORE_TOKENS = 256
 VECTOR_PIECES = ((512, 320), (832, 192))
@@ -51,10 +50,10 @@ def tile_routed_moe_kernel(tc, xT, w_words, w_scales, b, gate, offs, pos1, pos2,
         low = keep.tile([P, T], U32, name="low", align_bytes=64)
         row2 = keep.tile([P, 2 * T], BF16, name="row2", align_bytes=64)
         row3 = keep.tile([P, 2 * T], BF16, name="row3", align_bytes=64)
-        early = keep.tile([P, 2, 2, PIECE], U32, name="early", align_bytes=64)
-        late = turns.tile([P, 2, 2, PIECE], U32, name="late", tag="turns", align_bytes=64)
-        pairs = [early[:, 0, :, :], early[:, 1, :, :], late[:, 0, :, :], late[:, 1, :, :]]
-        fresh = keep.tile([P, 2, 2 * PIECE], U32, name="fresh", align_bytes=64)
+        first_pairs = keep.tile([P, 2, 2, PIECE], U32, name="first_pairs", align_bytes=64)
+        late_pairs = turns.tile([P, 2, 2, PIECE], U32, name="late_pairs", tag="turns", align_bytes=64)
+        pairs = [first_pairs[:, 0, :, :], first_pairs[:, 1, :, :], late_pairs[:, 0, :, :], late_pairs[:, 1, :, :]]
+        first_grouped = keep.tile([P, 2, 2 * PIECE], U32, name="first_grouped", align_bytes=64)
         s_words = keep.tile([P, SLOTS], U32, name="s_words", align_bytes=64)
         s_scales = keep.tile([P, SLOTS], U8, name="s_scales", align_bytes=64)
         w_sb = keep.tile([P, E, N * PACK], U8, name="w_sb", align_bytes=64)
@@ -72,13 +71,14 @@ def tile_routed_moe_kernel(tc, xT, w_words, w_scales, b, gate, offs, pos1, pos2,
         x_rows = xT.rearrange("(p j) t -> p j t", j=PACK)
         nc.sync.dma_start(out=raw[:, 2, :], in_=x_rows[:, 2, :])
         nc.sync.dma_start(offs_sb[:], offs)
-        raw3 = late[:].rearrange("p i u n -> p (i u n)")[:, PIECE : 3 * PIECE].bitcast(F32)
+        raw3 = late_pairs[:].rearrange("p i u n -> p (i u n)")[:, PIECE : PIECE + T].bitcast(F32)
         nc.sync.dma_start(out=raw3, in_=x_rows[:, 3, :])
-        raw_flat = raw[:].rearrange("p j t -> p (j t)")
-        x_flat = xT.rearrange("(p j) t -> p (j t)", j=PACK)
-        cut = T + PAIR_LOADS[1][0]
-        nc.sync.dma_start(out=raw_flat[:, 0:cut], in_=x_flat[:, 0:cut])
-        nc.sync.dma_start(out=raw_flat[:, cut : 2 * T], in_=x_flat[:, cut : 2 * T])
+        run = T + ROW1_PIECES[0][1]
+        nc.sync.dma_start(
+            out=raw[:].rearrange("p j t -> p (j t)")[:, 0:run], in_=xT.rearrange("(p j) t -> p (j t)", j=PACK)[:, 0:run]
+        )
+        for t0, n in ROW1_PIECES[1:]:
+            nc.sync.dma_start(out=raw[:, 1, t0 : t0 + n], in_=x_rows[:, 1, t0 : t0 + n])
         for g in range(4):
             nc.sync.dma_start(
                 out=ws_sb[32 * g : 32 * g + 4, :, :].bitcast(I32),
@@ -93,29 +93,40 @@ def tile_routed_moe_kernel(tc, xT, w_words, w_scales, b, gate, offs, pos1, pos2,
         def slots_of(j0, n):
             return offs_sb[:, j0 // LIST : (j0 + n) // LIST]
 
-        high_early = early[:, :, 1, :].bitcast(BF16).rearrange("p i (n e) -> p i n e", e=2)
-        high_late = late[:, :, 1, :].bitcast(BF16).rearrange("p i (n e) -> p i n e", e=2)
-        grouped = [fresh[:, 0, :], fresh[:, 1, :]] + [pairs[i].rearrange("p u n -> p (u n)") for i in range(2)]
+        first_high = first_pairs[:, :, 1, :].bitcast(BF16).rearrange("p i (n e) -> p i n e", e=2)
+        late_high = late_pairs[:, :, 1, :].bitcast(BF16).rearrange("p i (n e) -> p i n e", e=2)
 
-        def round_pairs(t0, n):
+        nc.scalar.copy(out=row2[:, ROW2_CUT:T], in_=raw[:, 2, ROW2_CUT:T])
+        nc.vector.tensor_copy(out=row2[:, 0:ROW2_CUT], in_=raw[:, 2, 0:ROW2_CUT])
+        nc.gpsimd.tensor_copy(out=row3[:, 0:T], in_=raw3)
+        for e, window in enumerate((raw[:, 2, :], raw3)):
+            nc.vector.tensor_copy(out=late_high[:, 1, :, e], in_=window.indirect(slots_of(3 * PIECE, PIECE)))
+        for e, window in enumerate((row2, row3)):
+            nc.scalar.activation(first_high[:, :, :, e], window[:].indirect(slots_of(0, 2 * PIECE)), COPY)
+        for e, window in enumerate((row2, row3)):
+            nc.scalar.activation(late_high[:, 0, :, e], window[:].indirect(slots_of(2 * PIECE, PIECE)), COPY)
+
+        for t0, n in ROW1_PIECES:
             nc.vector.tensor_copy(
                 out=low[:, t0 : t0 + n].bitcast(BF16).rearrange("p (n j) -> p n j", j=2),
                 in_=raw[:, 0:2, t0 : t0 + n].rearrange("p j n -> p n j"),
             )
+        for i in range(PIECES):
+            nc.vector.tensor_copy(out=pairs[i][:, 0, :], in_=low[:].indirect(slots_of(i * PIECE, PIECE)))
 
-        def side_by_side(copy, dtype, i, c0, n):
-            copy(
-                out=grouped[i][:, 2 * c0 : 2 * (c0 + n)].bitcast(dtype).rearrange("p (n u) -> p n u", u=2),
-                in_=pairs[i][:, :, c0 : c0 + n].bitcast(dtype).rearrange("p u n -> p n u"),
-            )
+        grouped = [first_grouped[:, 0, :], first_grouped[:, 1, :]] + [pairs[i].rearrange("p u n -> p (u n)") for i in range(2)]
+        for i in range(PIECES):
+            copy = nc.gpsimd.tensor_copy if i < 2 else nc.scalar.copy
+            copy(out=grouped[i].rearrange("p (n u) -> p n u", u=2), in_=pairs[i].rearrange("p u n -> p n u"))
 
+        y = turns.tile([P, SLOTS], F32, name="y", tag="turns", align_bytes=64)
         for_vector = []
-
-        def quantise_and_multiply(j0, n):
+        for j0, n in QUANTISE_PIECES:
+            c0 = j0 % PIECE
             nc.vector.quantize_mx(
                 out=s_words[:, j0 : j0 + n].bitcast(FP8X4),
                 scales=s_scales[:, j0 : j0 + n],
-                in_=grouped[j0 // PIECE][:, 2 * (j0 % PIECE) : 2 * (j0 % PIECE + n)].bitcast(BF16),
+                in_=grouped[j0 // PIECE][:, 2 * c0 : 2 * (c0 + n)].bitcast(BF16),
             )
             for e in range(j0 // C, (j0 + n - 1) // C + 1):
                 lo, hi = max(j0, e * C), min(j0 + n, (e + 1) * C)
@@ -129,38 +140,12 @@ def tile_routed_moe_kernel(tc, xT, w_words, w_scales, b, gate, offs, pos1, pos2,
                     start=True,
                     stop=True,
                 )
-                if lo in VECTOR_EMPTIES:
-                    for_vector.append((lo, hi, acc, e))
+                if e in VECTOR_EMPTIES:
+                    for_vector.append((e, acc))
                 else:
                     nc.scalar.activation(y[:, lo:hi], acc[:], RELU, bias=b_sb[:, e : e + 1])
-
-        nc.scalar.copy(out=row2[:, ROW2_CUT:T], in_=raw[:, 2, ROW2_CUT:T])
-        nc.vector.tensor_copy(out=row2[:, 0:ROW2_CUT], in_=raw[:, 2, 0:ROW2_CUT])
-        nc.gpsimd.tensor_copy(out=row3[:, 0:T], in_=raw3)
-        for row, window in ((0, raw[:, 2, :]), (1, raw3)):
-            nc.vector.tensor_copy(out=high_late[:, 1, :, row], in_=window.indirect(slots_of(3 * PIECE, PIECE)))
-        for row, window in ((0, row2), (1, row3)):
-            nc.scalar.activation(high_early[:, :, :, row], window[:].indirect(slots_of(0, 2 * PIECE)), COPY)
-        for row, window in ((0, row2), (1, row3)):
-            nc.scalar.activation(high_late[:, 0, :, row], window[:].indirect(slots_of(2 * PIECE, PIECE)), COPY)
-        for t0, n in PAIR_LOADS:
-            round_pairs(t0, n)
-        for i in range(PIECES):
-            nc.vector.tensor_copy(out=pairs[i][:, 0, :], in_=low[:, 0:T].indirect(slots_of(i * PIECE, PIECE)))
-        side_by_side(nc.gpsimd.tensor_copy, U32, 0, 0, PIECE)
-        side_by_side(nc.gpsimd.tensor_copy, U32, 1, 0, 384)
-        side_by_side(nc.scalar.copy, U32, 1, 384, 128)
-        for i in range(2, 4):
-            side_by_side(nc.scalar.copy, U32, i, 0, PIECE)
-        y = turns.tile([P, SLOTS], F32, name="y", tag="turns", align_bytes=64)
-        quantise_and_multiply(0, 512)
-        quantise_and_multiply(512, 512)
-        quantise_and_multiply(1024, 512)
-        quantise_and_multiply(1536, 256)
-        quantise_and_multiply(1792, 128)
-        quantise_and_multiply(1920, 128)
-        for lo, hi, acc, e in for_vector:
-            nc.vector.tensor_scalar(y[:, lo:hi], acc[:], b_sb[:, e : e + 1], 0.0, ADD, MAX)
+        for e, acc in for_vector:
+            nc.vector.tensor_scalar(y[:, e * C : (e + 1) * C], acc[:], b_sb[:, e : e + 1], 0.0, ADD, MAX)
 
         def gated(pool, pos_sb, gate_sb, t0, n, name):
             part = pool.tile([P, n], F32, name=name)

@@ -26,6 +26,8 @@ FLOPS = 2 * K * N * SLOTS
 
 PIECE = 512
 PIECES = SLOTS // PIECE
+HALF = SLOTS // 2
+EARLY = 544
 ROW2_CUT = 688
 ROW1_PIECES = ((0, 384), (384, 384), (768, 256))
 QUANTISE_PIECES = ((0, 512), (512, 512), (1024, 512), (1536, 256), (1792, 128), (1920, 128))
@@ -51,8 +53,9 @@ def tile_routed_moe_kernel(tc, xT, w_words, w_scales, b, gate, offs, pos1, pos2,
         row2 = keep.tile([P, 2 * T], BF16, name="row2", align_bytes=64)
         row3 = keep.tile([P, 2 * T], BF16, name="row3", align_bytes=64)
         first_pairs = keep.tile([P, 2, 2, PIECE], U32, name="first_pairs", align_bytes=64)
-        late_pairs = turns.tile([P, 2, 2, PIECE], U32, name="late_pairs", tag="turns", align_bytes=64)
-        pairs = [first_pairs[:, 0, :, :], first_pairs[:, 1, :, :], late_pairs[:, 0, :, :], late_pairs[:, 1, :, :]]
+        late = turns.tile([P, SLOTS + EARLY], U32, name="late", tag="turns", align_bytes=64)
+        late_pairs = late[:, 0:SLOTS].rearrange("p (u n) -> p u n", u=2)
+        pairs = [first_pairs[:, 0, :, :], first_pairs[:, 1, :, :], late_pairs[:, :, 0:PIECE], late_pairs[:, :, PIECE:HALF]]
         first_grouped = keep.tile([P, 2, 2 * PIECE], U32, name="first_grouped", align_bytes=64)
         s_words = keep.tile([P, SLOTS], U32, name="s_words", align_bytes=64)
         s_scales = keep.tile([P, SLOTS], U8, name="s_scales", align_bytes=64)
@@ -71,7 +74,7 @@ def tile_routed_moe_kernel(tc, xT, w_words, w_scales, b, gate, offs, pos1, pos2,
         x_rows = xT.rearrange("(p j) t -> p j t", j=PACK)
         nc.sync.dma_start(out=raw[:, 2, :], in_=x_rows[:, 2, :])
         nc.sync.dma_start(offs_sb[:], offs)
-        raw3 = late_pairs[:].rearrange("p i u n -> p (i u n)")[:, PIECE : PIECE + T].bitcast(F32)
+        raw3 = late[:, HALF + EARLY : HALF + EARLY + T].bitcast(F32)
         nc.sync.dma_start(out=raw3, in_=x_rows[:, 3, :])
         run = T + ROW1_PIECES[0][1]
         nc.sync.dma_start(
@@ -94,17 +97,17 @@ def tile_routed_moe_kernel(tc, xT, w_words, w_scales, b, gate, offs, pos1, pos2,
             return offs_sb[:, j0 // LIST : (j0 + n) // LIST]
 
         first_high = first_pairs[:, :, 1, :].bitcast(BF16).rearrange("p i (n e) -> p i n e", e=2)
-        late_high = late_pairs[:, :, 1, :].bitcast(BF16).rearrange("p i (n e) -> p i n e", e=2)
+        late_high = late_pairs[:, 1, :].bitcast(BF16).rearrange("p (n e) -> p n e", e=2)
 
         nc.scalar.copy(out=row2[:, ROW2_CUT:T], in_=raw[:, 2, ROW2_CUT:T])
         nc.vector.tensor_copy(out=row2[:, 0:ROW2_CUT], in_=raw[:, 2, 0:ROW2_CUT])
         nc.gpsimd.tensor_copy(out=row3[:, 0:T], in_=raw3)
         for e, window in enumerate((raw[:, 2, :], raw3)):
-            nc.vector.tensor_copy(out=late_high[:, 1, :, e], in_=window.indirect(slots_of(3 * PIECE, PIECE)))
+            nc.vector.tensor_copy(out=late_high[:, 0:EARLY, e], in_=window.indirect(slots_of(HALF, EARLY)))
         for e, window in enumerate((row2, row3)):
             nc.scalar.activation(first_high[:, :, :, e], window[:].indirect(slots_of(0, 2 * PIECE)), COPY)
         for e, window in enumerate((row2, row3)):
-            nc.scalar.activation(late_high[:, 0, :, e], window[:].indirect(slots_of(2 * PIECE, PIECE)), COPY)
+            nc.scalar.activation(late_high[:, EARLY:HALF, e], window[:].indirect(slots_of(HALF + EARLY, HALF - EARLY)), COPY)
 
         for t0, n in ROW1_PIECES:
             nc.vector.tensor_copy(

@@ -32,9 +32,10 @@ ROW2_CUT = 688
 ROW1_PIECES = ((0, 384), (384, 384), (768, 256))
 QUANTISE_PIECES = ((0, 512), (512, 512), (1024, 512), (1536, 256), (1792, 128), (1920, 128))
 VECTOR_EMPTIES = (3, 6)
-TENSOR_TOKENS = 512
-STORE_TOKENS = 256
-VECTOR_PIECES = ((512, 320), (832, 192))
+SCALAR_TOKENS = 768
+SCALAR_PIECES = ((0, 512), (512, 256))
+TURN_TOKENS = 256
+STORE_PIECES = ((0, 256), (256, 256), (512, 128), (640, 128))
 
 
 def tile_routed_moe_kernel(tc, xT, w_words, w_scales, b, gate, offs, pos1, pos2, out):
@@ -62,8 +63,9 @@ def tile_routed_moe_kernel(tc, xT, w_words, w_scales, b, gate, offs, pos1, pos2,
         w_sb = keep.tile([P, E, N * PACK], U8, name="w_sb", align_bytes=64)
         ws_sb = keep.tile([P, E, N], U8, name="ws_sb", align_bytes=64)
         b_sb = keep.tile([P, E], F32, name="b_sb")
-        gates = keep.tile([P, 2, T], F32, name="gates")
-        gate1_sb, gate2_sb = gates[:, 0, :], gates[:, 1, :]
+        gate1_sb = keep.tile([P, T], F32, name="gate1_sb")
+        gate2_sb = keep.tile([P, T - SCALAR_TOKENS], F32, name="gate2_sb")
+        gate2_cols = keep.tile([P, SCALAR_TOKENS // P], F32, name="gate2_cols")
         ident = keep.tile([P, P], F32, name="ident")
         make_identity(nc, ident[:])
 
@@ -91,7 +93,10 @@ def tile_routed_moe_kernel(tc, xT, w_words, w_scales, b, gate, offs, pos1, pos2,
         nc.sync.dma_start(out=b_sb[:], in_=b)
         nc.sync.dma_start(pos1_sb[:], pos1)
         nc.sync.dma_start(pos2_sb[:], pos2)
-        nc.sync.dma_start(out=gates[:], in_=gate.rearrange("g n t -> n g t"))
+        nc.sync.dma_start(out=gate1_sb[:], in_=gate[0])
+        nc.sync.dma_start(out=gate2_sb[:], in_=gate[1, :, SCALAR_TOKENS:T])
+        with nc.allow_non_contiguous_dma(reason="one weight a partition"):
+            nc.sync.dma_start(out=gate2_cols[:], in_=gate[1, 0, 0:SCALAR_TOKENS].rearrange("(c p) -> p c", p=P))
 
         def slots_of(j0, n):
             return offs_sb[:, j0 // LIST : (j0 + n) // LIST]
@@ -150,44 +155,36 @@ def tile_routed_moe_kernel(tc, xT, w_words, w_scales, b, gate, offs, pos1, pos2,
         for e, acc in for_vector:
             nc.vector.tensor_scalar(y[:, e * C : (e + 1) * C], acc[:], b_sb[:, e : e + 1], 0.0, ADD, MAX)
 
-        def gated(pool, pos_sb, gate_sb, t0, n, name):
-            part = pool.tile([P, n], F32, name=name)
-            nc.vector.tensor_tensor(
-                part[:], y[:].indirect(pos_sb[:, t0 // LIST : (t0 + n) // LIST]), gate_sb[:, t0 : t0 + n], MULT
-            )
-            return part
+        def results(pos_sb, t0, n):
+            return y[:].indirect(pos_sb[:, t0 // LIST : (t0 + n) // LIST])
 
-        blocks = range(0, TENSOR_TOKENS, P)
-        first = gated(keep, pos1_sb, gate1_sb, 0, TENSOR_TOKENS, "first")
-        turned = [psum.tile([P, P], F32, name="bank") for c0 in blocks]
-        for c0, bank in zip(blocks, turned):
-            nc.tensor.matmul(bank[:], first[:, c0 : c0 + P], ident[:], start=True, stop=False, is_transpose=True)
-        second = gated(keep, pos2_sb, gate2_sb, 0, TENSOR_TOKENS, "second")
-        turned_sb = []
-        for c0, bank in zip(blocks, turned):
-            nc.tensor.matmul(bank[:], second[:, c0 : c0 + P], ident[:], start=False, stop=True, is_transpose=True)
-            held = stage.tile([P, P], F32, name="held", bufs=len(blocks))
-            nc.scalar.copy(out=held[:], in_=bank[:])
-            turned_sb.append(held)
-        for t0 in range(0, TENSOR_TOKENS, STORE_TOKENS):
-            back = psum.tile([P, STORE_TOKENS], F32, name="bank")
-            for c0 in range(0, STORE_TOKENS, P):
-                nc.tensor.transpose(back[:, c0 : c0 + P], turned_sb[(t0 + c0) // P][:], ident[:])
-            summed = stage.tile([P, STORE_TOKENS], F32, name="summed")
-            nc.scalar.copy(out=summed[:], in_=back[:])
-            nc.scalar.dma_start(out=out[:, t0 : t0 + STORE_TOKENS], in_=summed[:])
+        first = keep.tile([P, T], F32, name="first")
+        nc.vector.tensor_tensor(first[:], results(pos1_sb, 0, T), gate1_sb[:], MULT)
+        rest = T - SCALAR_TOKENS
+        second_rest = keep.tile([P, rest], F32, name="second_rest")
+        nc.vector.tensor_tensor(second_rest[:], results(pos2_sb, SCALAR_TOKENS, rest), gate2_sb[:], MULT)
 
-        part1 = gated(keep, pos1_sb, gate1_sb, TENSOR_TOKENS, T - TENSOR_TOKENS, "part1")
+        total_rest = keep.tile([P, rest], F32, name="total_rest")
+        nc.gpsimd.tensor_tensor(total_rest[:], first[:, SCALAR_TOKENS:T], second_rest[:], ADD)
+        nc.sync.dma_start(out=out[:, SCALAR_TOKENS:T], in_=total_rest[:])
 
-        def add_and_store(t0, n, part2):
+        second = keep.tile([P, SCALAR_TOKENS], F32, name="second")
+        turned = []
+        for t0, n in SCALAR_PIECES:
+            nc.scalar.activation(second[:, t0 : t0 + n], results(pos2_sb, t0, n), COPY)
+            for b0 in range(t0, t0 + n, TURN_TOKENS):
+                bank = psum.tile([P, TURN_TOKENS], F32, name="bank")
+                for c0 in range(0, TURN_TOKENS, P):
+                    nc.tensor.transpose(bank[:, c0 : c0 + P], second[:, b0 + c0 : b0 + c0 + P], ident[:])
+                    turned.append(bank[:, c0 : c0 + P])
+
+        weighed = keep.tile([P, SCALAR_TOKENS], F32, name="weighed")
+        for t0, n in STORE_PIECES:
+            back = psum.tile([P, n], F32, name="bank")
+            for c0 in range(t0, t0 + n, P):
+                c = c0 // P
+                nc.scalar.activation(weighed[:, c0 : c0 + P], turned[c], COPY, scale=gate2_cols[:, c : c + 1])
+                nc.tensor.transpose(back[:, c0 - t0 : c0 - t0 + P], weighed[:, c0 : c0 + P], ident[:])
             total = stage.tile([P, n], F32, name="total")
-            nc.vector.tensor_tensor(total[:], part1[:, t0 - TENSOR_TOKENS : t0 - TENSOR_TOKENS + n], part2[:], ADD)
+            nc.vector.tensor_tensor(total[:], back[:], first[:, t0 : t0 + n], ADD)
             nc.sync.dma_start(out=out[:, t0 : t0 + n], in_=total[:])
-
-        to_add = None
-        for t0, n in VECTOR_PIECES:
-            part2 = gated(stage, pos2_sb, gate2_sb, t0, n, "part2")
-            if to_add is not None:
-                add_and_store(*to_add)
-            to_add = (t0, n, part2)
-        add_and_store(*to_add)

@@ -32,10 +32,11 @@ ROW2_CUT = 688
 ROW1_PIECES = ((0, 384), (384, 384), (768, 256))
 QUANTISE_PIECES = ((0, 512), (512, 512), (1024, 512), (1536, 256), (1792, 128), (1920, 128))
 VECTOR_EMPTIES = (3, 6)
-SCALAR_TOKENS = 768
-SCALAR_PIECES = ((0, 512), (512, 256))
+VECTOR_TOKENS = 256
+SCALAR_TOKENS = T - VECTOR_TOKENS
+SCALAR_PIECES = ((256, 512), (768, 256))
 TURN_TOKENS = 256
-STORE_PIECES = ((0, 256), (256, 256), (512, 128), (640, 128))
+FINISH_ORDER = (512, 256, 768)
 
 
 def tile_routed_moe_kernel(tc, xT, w_words, w_scales, b, gate, offs, pos1, pos2, out):
@@ -64,7 +65,7 @@ def tile_routed_moe_kernel(tc, xT, w_words, w_scales, b, gate, offs, pos1, pos2,
         ws_sb = keep.tile([P, E, N], U8, name="ws_sb", align_bytes=64)
         b_sb = keep.tile([P, E], F32, name="b_sb")
         gate1_sb = keep.tile([P, T], F32, name="gate1_sb")
-        gate2_sb = keep.tile([P, T - SCALAR_TOKENS], F32, name="gate2_sb")
+        gate2_sb = keep.tile([P, VECTOR_TOKENS], F32, name="gate2_sb")
         gate2_cols = keep.tile([P, SCALAR_TOKENS // P], F32, name="gate2_cols")
         ident = keep.tile([P, P], F32, name="ident")
         make_identity(nc, ident[:])
@@ -94,9 +95,9 @@ def tile_routed_moe_kernel(tc, xT, w_words, w_scales, b, gate, offs, pos1, pos2,
         nc.sync.dma_start(pos1_sb[:], pos1)
         nc.sync.dma_start(pos2_sb[:], pos2)
         nc.sync.dma_start(out=gate1_sb[:], in_=gate[0])
-        nc.sync.dma_start(out=gate2_sb[:], in_=gate[1, :, SCALAR_TOKENS:T])
+        nc.sync.dma_start(out=gate2_sb[:], in_=gate[1, :, 0:VECTOR_TOKENS])
         with nc.allow_non_contiguous_dma(reason="one weight a partition"):
-            nc.sync.dma_start(out=gate2_cols[:], in_=gate[1, 0, 0:SCALAR_TOKENS].rearrange("(c p) -> p c", p=P))
+            nc.sync.dma_start(out=gate2_cols[:], in_=gate[1, 0, VECTOR_TOKENS:T].rearrange("(c p) -> p c", p=P))
 
         def slots_of(j0, n):
             return offs_sb[:, j0 // LIST : (j0 + n) // LIST]
@@ -160,31 +161,30 @@ def tile_routed_moe_kernel(tc, xT, w_words, w_scales, b, gate, offs, pos1, pos2,
 
         first = keep.tile([P, T], F32, name="first")
         nc.vector.tensor_tensor(first[:], results(pos1_sb, 0, T), gate1_sb[:], MULT)
-        rest = T - SCALAR_TOKENS
-        second_rest = keep.tile([P, rest], F32, name="second_rest")
-        nc.vector.tensor_tensor(second_rest[:], results(pos2_sb, SCALAR_TOKENS, rest), gate2_sb[:], MULT)
+        second = keep.tile([P, T], F32, name="second")
+        nc.vector.tensor_tensor(second[:, 0:VECTOR_TOKENS], results(pos2_sb, 0, VECTOR_TOKENS), gate2_sb[:], MULT)
+        total = keep.tile([P, T], F32, name="total")
+        nc.gpsimd.tensor_tensor(total[:, 0:VECTOR_TOKENS], first[:, 0:VECTOR_TOKENS], second[:, 0:VECTOR_TOKENS], ADD)
 
-        total_rest = keep.tile([P, rest], F32, name="total_rest")
-        nc.gpsimd.tensor_tensor(total_rest[:], first[:, SCALAR_TOKENS:T], second_rest[:], ADD)
-        nc.sync.dma_start(out=out[:, SCALAR_TOKENS:T], in_=total_rest[:])
-
-        second = keep.tile([P, SCALAR_TOKENS], F32, name="second")
-        turned = []
+        turned = {}
         for t0, n in SCALAR_PIECES:
             nc.scalar.activation(second[:, t0 : t0 + n], results(pos2_sb, t0, n), COPY)
-            for b0 in range(t0, t0 + n, TURN_TOKENS):
-                bank = psum.tile([P, TURN_TOKENS], F32, name="bank")
-                for c0 in range(0, TURN_TOKENS, P):
-                    nc.tensor.transpose(bank[:, c0 : c0 + P], second[:, b0 + c0 : b0 + c0 + P], ident[:])
-                    turned.append(bank[:, c0 : c0 + P])
+            for b0 in FINISH_ORDER:
+                if t0 <= b0 < t0 + n:
+                    bank = psum.tile([P, TURN_TOKENS], F32, name="bank")
+                    for c0 in range(0, TURN_TOKENS, P):
+                        nc.tensor.transpose(bank[:, c0 : c0 + P], second[:, b0 + c0 : b0 + c0 + P], ident[:])
+                    turned[b0] = bank
 
-        weighed = keep.tile([P, SCALAR_TOKENS], F32, name="weighed")
-        for t0, n in STORE_PIECES:
-            back = psum.tile([P, n], F32, name="bank")
-            for c0 in range(t0, t0 + n, P):
-                c = c0 // P
-                nc.scalar.activation(weighed[:, c0 : c0 + P], turned[c], COPY, scale=gate2_cols[:, c : c + 1])
-                nc.tensor.transpose(back[:, c0 - t0 : c0 - t0 + P], weighed[:, c0 : c0 + P], ident[:])
-            total = stage.tile([P, n], F32, name="total")
-            nc.vector.tensor_tensor(total[:], back[:], first[:, t0 : t0 + n], ADD)
-            nc.sync.dma_start(out=out[:, t0 : t0 + n], in_=total[:])
+        weighed = keep.tile([P, T], F32, name="weighed")
+        for b0 in FINISH_ORDER:
+            back = psum.tile([P, TURN_TOKENS], F32, name="bank")
+            for c0 in range(0, TURN_TOKENS, P):
+                t0 = b0 + c0
+                c = (t0 - VECTOR_TOKENS) // P
+                nc.scalar.activation(weighed[:, t0 : t0 + P], turned[b0][:, c0 : c0 + P], COPY, scale=gate2_cols[:, c : c + 1])
+                nc.tensor.transpose(back[:, c0 : c0 + P], weighed[:, t0 : t0 + P], ident[:])
+            end = b0 + TURN_TOKENS
+            nc.vector.tensor_tensor(total[:, b0:end], back[:], first[:, b0:end], ADD)
+            start = 0 if b0 == VECTOR_TOKENS else b0
+            nc.sync.dma_start(out=out[:, start:end], in_=total[:, start:end])

@@ -34,9 +34,8 @@ QUANTISE_PIECES = ((0, 512), (512, 512), (1024, 512), (1536, 256), (1792, 128), 
 VECTOR_EMPTIES = (3, 6)
 VECTOR_TOKENS = 256
 SCALAR_TOKENS = T - VECTOR_TOKENS
-SCALAR_PIECES = ((256, 512), (768, 256))
-TURN_TOKENS = 256
-FINISH_ORDER = (512, 256, 768)
+SCALAR_STEPS = ((512, 384, 0), (256, 256, 2), (896, 128, 4))
+FINISH = ((512, 256, (512, 256)), (256, 256, (0, 512)), (768, 128, None), (896, 128, (768, 256)))
 
 
 def tile_routed_moe_kernel(tc, xT, w_words, w_scales, b, gate, offs, pos1, pos2, out):
@@ -70,9 +69,18 @@ def tile_routed_moe_kernel(tc, xT, w_words, w_scales, b, gate, offs, pos1, pos2,
         ident = keep.tile([P, P], F32, name="ident")
         make_identity(nc, ident[:])
 
+        gate2_rows = keep.tile([P, P], F32, name="gate2_rows")
+        nc.vector.memset(gate2_rows[:], 0.0)
         nc.vector.memset(row2[:, T : 2 * T].bitcast(I32), 0)
         nc.vector.memset(row3[:, T : 2 * T].bitcast(I32), 0)
         nc.vector.memset(ws_sb[:].rearrange("p e n -> p (e n)").bitcast(I32), 0)
+
+        blocks = gate[1, 0, VECTOR_TOKENS:T].rearrange("(c p) -> c p", p=P)
+        for c0, c1 in ((0, 4), (4, 6)):
+            nc.scalar.dma_start(out=gate2_rows[c0:c1, :], in_=blocks[c0:c1, :])
+        gate_bank = psum.tile([P, P], F32, name="bank")
+        nc.tensor.transpose(gate_bank[:], gate2_rows[:], ident[:])
+        nc.scalar.copy(out=gate2_cols[:], in_=gate_bank[:, 0 : SCALAR_TOKENS // P])
 
         x_rows = xT.rearrange("(p j) t -> p j t", j=PACK)
         nc.sync.dma_start(out=raw[:, 2, :], in_=x_rows[:, 2, :])
@@ -96,8 +104,6 @@ def tile_routed_moe_kernel(tc, xT, w_words, w_scales, b, gate, offs, pos1, pos2,
         nc.sync.dma_start(pos2_sb[:], pos2)
         nc.sync.dma_start(out=gate1_sb[:], in_=gate[0])
         nc.sync.dma_start(out=gate2_sb[:], in_=gate[1, :, 0:VECTOR_TOKENS])
-        with nc.allow_non_contiguous_dma(reason="one weight a partition"):
-            nc.sync.dma_start(out=gate2_cols[:], in_=gate[1, 0, VECTOR_TOKENS:T].rearrange("(c p) -> p c", p=P))
 
         def slots_of(j0, n):
             return offs_sb[:, j0 // LIST : (j0 + n) // LIST]
@@ -166,25 +172,30 @@ def tile_routed_moe_kernel(tc, xT, w_words, w_scales, b, gate, offs, pos1, pos2,
         total = keep.tile([P, T], F32, name="total")
         nc.gpsimd.tensor_tensor(total[:, 0:VECTOR_TOKENS], first[:, 0:VECTOR_TOKENS], second[:, 0:VECTOR_TOKENS], ADD)
 
+        order = [t0 for b0, n, stored in FINISH for t0 in range(b0, b0 + n, P)]
         turned = {}
-        for t0, n in SCALAR_PIECES:
-            nc.scalar.activation(second[:, t0 : t0 + n], results(pos2_sb, t0, n), COPY)
-            for b0 in FINISH_ORDER:
-                if t0 <= b0 < t0 + n:
-                    bank = psum.tile([P, TURN_TOKENS], F32, name="bank")
-                    for c0 in range(0, TURN_TOKENS, P):
-                        nc.tensor.transpose(bank[:, c0 : c0 + P], second[:, b0 + c0 : b0 + c0 + P], ident[:])
-                    turned[b0] = bank
-
         weighed = keep.tile([P, T], F32, name="weighed")
-        for b0 in FINISH_ORDER:
-            back = psum.tile([P, TURN_TOKENS], F32, name="bank")
-            for c0 in range(0, TURN_TOKENS, P):
-                t0 = b0 + c0
+        backs = {}
+        done = 0
+        for g0, gn, count in SCALAR_STEPS:
+            nc.scalar.activation(second[:, g0 : g0 + gn], results(pos2_sb, g0, gn), COPY)
+            for b0 in range(g0, g0 + gn, 2 * P):
+                width = min(2 * P, g0 + gn - b0)
+                bank = psum.tile([P, width], F32, name="bank")
+                for c0 in range(0, width, P):
+                    nc.tensor.transpose(bank[:, c0 : c0 + P], second[:, b0 + c0 : b0 + c0 + P], ident[:])
+                    turned[b0 + c0] = bank[:, c0 : c0 + P]
+            for t0 in order[done : done + count]:
                 c = (t0 - VECTOR_TOKENS) // P
-                nc.scalar.activation(weighed[:, t0 : t0 + P], turned[b0][:, c0 : c0 + P], COPY, scale=gate2_cols[:, c : c + 1])
-                nc.tensor.transpose(back[:, c0 : c0 + P], weighed[:, t0 : t0 + P], ident[:])
-            end = b0 + TURN_TOKENS
-            nc.vector.tensor_tensor(total[:, b0:end], back[:], first[:, b0:end], ADD)
-            start = 0 if b0 == VECTOR_TOKENS else b0
-            nc.sync.dma_start(out=out[:, start:end], in_=total[:, start:end])
+                nc.scalar.activation(weighed[:, t0 : t0 + P], turned[t0], COPY, scale=gate2_cols[:, c : c + 1])
+                for b0, n, stored in FINISH:
+                    if b0 <= t0 < b0 + n:
+                        if t0 == b0:
+                            backs[b0] = psum.tile([P, n], F32, name="bank")
+                        nc.tensor.transpose(backs[b0][:, t0 - b0 : t0 - b0 + P], weighed[:, t0 : t0 + P], ident[:])
+                        if t0 + P == b0 + n:
+                            nc.vector.tensor_tensor(total[:, b0 : b0 + n], backs[b0][:], first[:, b0 : b0 + n], ADD)
+                            if stored is not None:
+                                s0, sn = stored
+                                nc.sync.dma_start(out=out[:, s0 : s0 + sn], in_=total[:, s0 : s0 + sn])
+            done += count

@@ -28,7 +28,8 @@ PIECE = 512
 PIECES = SLOTS // PIECE
 HALF = SLOTS // 2
 EARLY = 544
-ROW2_CUT = 688
+ROW2_CUT = 768
+ROW2_SCALAR = 256
 ROW1_PIECES = ((0, 384), (384, 384), (768, 256))
 QUANTISE_PIECES = ((0, 512), (512, 512), (1024, 512), (1536, 256), (1792, 128), (1920, 128))
 VECTOR_EMPTIES = (3, 6)
@@ -83,8 +84,9 @@ def tile_routed_moe_kernel(tc, xT, w_words, w_scales, b, gate, offs, pos1, pos2,
         nc.scalar.copy(out=gate2_cols[:], in_=gate_bank[:, 0 : SCALAR_TOKENS // P])
 
         x_rows = xT.rearrange("(p j) t -> p j t", j=PACK)
-        nc.sync.dma_start(out=raw[:, 2, :], in_=x_rows[:, 2, :])
+        nc.sync.dma_start(out=raw[:, 2, 0:ROW2_CUT], in_=x_rows[:, 2, 0:ROW2_CUT])
         nc.sync.dma_start(offs_sb[:], offs)
+        nc.sync.dma_start(out=raw[:, 2, ROW2_CUT:T], in_=x_rows[:, 2, ROW2_CUT:T])
         raw3 = late[:, HALF + EARLY : HALF + EARLY + T].bitcast(F32)
         nc.sync.dma_start(out=raw3, in_=x_rows[:, 3, :])
         run = T + ROW1_PIECES[0][1]
@@ -111,8 +113,9 @@ def tile_routed_moe_kernel(tc, xT, w_words, w_scales, b, gate, offs, pos1, pos2,
         first_high = first_pairs[:, :, 1, :].bitcast(BF16).rearrange("p i (n e) -> p i n e", e=2)
         late_high = late_pairs[:, 1, :].bitcast(BF16).rearrange("p (n e) -> p n e", e=2)
 
-        nc.scalar.copy(out=row2[:, ROW2_CUT:T], in_=raw[:, 2, ROW2_CUT:T])
-        nc.vector.tensor_copy(out=row2[:, 0:ROW2_CUT], in_=raw[:, 2, 0:ROW2_CUT])
+        nc.scalar.copy(out=row2[:, 0:ROW2_SCALAR], in_=raw[:, 2, 0:ROW2_SCALAR])
+        nc.vector.tensor_copy(out=row2[:, ROW2_SCALAR:ROW2_CUT], in_=raw[:, 2, ROW2_SCALAR:ROW2_CUT])
+        nc.vector.tensor_copy(out=row2[:, ROW2_CUT:T], in_=raw[:, 2, ROW2_CUT:T])
         nc.gpsimd.tensor_copy(out=row3[:, 0:T], in_=raw3)
         for e, window in enumerate((raw[:, 2, :], raw3)):
             nc.vector.tensor_copy(out=late_high[:, 0:EARLY, e], in_=window.indirect(slots_of(HALF, EARLY)))
@@ -123,8 +126,8 @@ def tile_routed_moe_kernel(tc, xT, w_words, w_scales, b, gate, offs, pos1, pos2,
 
         for t0, n in ROW1_PIECES:
             nc.vector.tensor_copy(
-                out=low[:, t0 : t0 + n].bitcast(BF16).rearrange("p (n j) -> p n j", j=2),
-                in_=raw[:, 0:2, t0 : t0 + n].rearrange("p j n -> p n j"),
+                out=low[:, t0 : t0 + n].bitcast(BF16).rearrange("p (c i j) -> p c j i", i=4, j=2),
+                in_=raw[:, 0:2, t0 : t0 + n].rearrange("p j (c i) -> p c j i", i=4),
             )
         for i in range(PIECES):
             nc.vector.tensor_copy(out=pairs[i][:, 0, :], in_=low[:].indirect(slots_of(i * PIECE, PIECE)))

@@ -24,14 +24,16 @@ MULT = mybir.AluOpType.mult
 
 FLOPS = 2 * K * N * SLOTS
 
-PIECE = 512
-PIECES = SLOTS // PIECE
-HALF = SLOTS // 2
-EARLY = 544
-ROW2_CUT = 768
-ROW2_SCALAR = 256
-ROW1_PIECES = ((0, 384), (384, 384), (768, 256))
-QUANTISE_PIECES = ((0, 512), (512, 512), (1024, 512), (1536, 256), (1792, 128), (1920, 128))
+BLOCK = 128
+ROW0_PIECES = ((0, 768), (768, 256))
+ROW1_PIECES = ((0, 512), (512, 512))
+SCALAR_LOW = (0, 512)
+VECTOR_LOW = ((512, 768), (1280, 768))
+SCALAR_HIGH = ((0, 256), (256, 512))
+VECTOR_HIGH = ((768, 512), (1280, 384), (1664, 384))
+GPSIMD_LAYS = ((0, 256), (256, 512))
+SCALAR_LAYS = ((768, 512), (1280, 384), (1664, 384))
+QUANTISE_PIECES = ((0, 256), (256, 256), (512, 512), (1024, 512), (1536, 256), (1792, 128), (1920, 128))
 VECTOR_EMPTIES = (3, 6)
 VECTOR_TOKENS = 256
 SCALAR_TOKENS = T - VECTOR_TOKENS
@@ -43,22 +45,18 @@ def tile_routed_moe_kernel(tc, xT, w_words, w_scales, b, gate, offs, pos1, pos2,
     nc = tc.nc
     with ExitStack() as ctx:
         keep = ctx.enter_context(tc.tile_pool(name="keep", bufs=1))
-        stage = ctx.enter_context(tc.tile_pool(name="stage", bufs=4))
         turns = ctx.enter_context(tc.tile_pool(name="turns", bufs=1))
         psum = ctx.enter_context(tc.psum_pool(name="psum", bufs=8))
 
         offs_sb = keep.tile([P, SLOTS // LIST], U16, name="offs_sb")
         pos1_sb = keep.tile([P, T // LIST], U16, name="pos1_sb")
         pos2_sb = keep.tile([P, T // LIST], U16, name="pos2_sb")
-        raw = keep.tile([P, PACK - 1, T], F32, name="raw")
+        rows = [keep.tile([P, T], F32, name="row%d" % j) for j in range(PACK - 1)]
+        rows.append(turns.tile([P, T], F32, name="row3", tag="row3"))
         low = keep.tile([P, T], U32, name="low", align_bytes=64)
-        row2 = keep.tile([P, 2 * T], BF16, name="row2", align_bytes=64)
-        row3 = keep.tile([P, 2 * T], BF16, name="row3", align_bytes=64)
-        first_pairs = keep.tile([P, 2, 2, PIECE], U32, name="first_pairs", align_bytes=64)
-        late = turns.tile([P, SLOTS + EARLY], U32, name="late", tag="turns", align_bytes=64)
-        late_pairs = late[:, 0:SLOTS].rearrange("p (u n) -> p u n", u=2)
-        pairs = [first_pairs[:, 0, :, :], first_pairs[:, 1, :, :], late_pairs[:, :, 0:PIECE], late_pairs[:, :, PIECE:HALF]]
-        first_grouped = keep.tile([P, 2, 2 * PIECE], U32, name="first_grouped", align_bytes=64)
+        high = keep.tile([P, T], U32, name="high", align_bytes=64)
+        pairs = turns.tile([P, SLOTS // BLOCK, 2, BLOCK], U32, name="pairs", tag="turns", align_bytes=64)
+        grouped = keep.tile([P, 2 * SLOTS], U32, name="grouped", align_bytes=64)
         s_words = keep.tile([P, SLOTS], U32, name="s_words", align_bytes=64)
         s_scales = keep.tile([P, SLOTS], U8, name="s_scales", align_bytes=64)
         w_sb = keep.tile([P, E, N * PACK], U8, name="w_sb", align_bytes=64)
@@ -66,35 +64,23 @@ def tile_routed_moe_kernel(tc, xT, w_words, w_scales, b, gate, offs, pos1, pos2,
         b_sb = keep.tile([P, E], F32, name="b_sb")
         gate1_sb = keep.tile([P, T], F32, name="gate1_sb")
         gate2_sb = keep.tile([P, VECTOR_TOKENS], F32, name="gate2_sb")
-        gate2_cols = keep.tile([P, SCALAR_TOKENS // P], F32, name="gate2_cols")
         ident = keep.tile([P, P], F32, name="ident")
         make_identity(nc, ident[:])
 
         gate2_rows = keep.tile([P, P], F32, name="gate2_rows")
-        nc.vector.memset(gate2_rows[:], 0.0)
-        nc.vector.memset(row2[:, T : 2 * T].bitcast(I32), 0)
-        nc.vector.memset(row3[:, T : 2 * T].bitcast(I32), 0)
+        nc.vector.memset(gate2_rows[:, 0 : P // 2], 0.0)
+        nc.scalar.copy(out=gate2_rows[:, P // 2 : P], in_=gate2_rows[:, 0 : P // 2])
         nc.vector.memset(ws_sb[:].rearrange("p e n -> p (e n)").bitcast(I32), 0)
 
-        blocks = gate[1, 0, VECTOR_TOKENS:T].rearrange("(c p) -> c p", p=P)
-        for c0, c1 in ((0, 4), (4, 6)):
-            nc.scalar.dma_start(out=gate2_rows[c0:c1, :], in_=blocks[c0:c1, :])
-        gate_bank = psum.tile([P, P], F32, name="bank")
-        nc.tensor.transpose(gate_bank[:], gate2_rows[:], ident[:])
-        nc.scalar.copy(out=gate2_cols[:], in_=gate_bank[:, 0 : SCALAR_TOKENS // P])
-
         x_rows = xT.rearrange("(p j) t -> p j t", j=PACK)
-        nc.sync.dma_start(out=raw[:, 2, 0:ROW2_CUT], in_=x_rows[:, 2, 0:ROW2_CUT])
-        nc.sync.dma_start(offs_sb[:], offs)
-        nc.sync.dma_start(out=raw[:, 2, ROW2_CUT:T], in_=x_rows[:, 2, ROW2_CUT:T])
-        raw3 = late[:, HALF + EARLY : HALF + EARLY + T].bitcast(F32)
-        nc.sync.dma_start(out=raw3, in_=x_rows[:, 3, :])
-        run = T + ROW1_PIECES[0][1]
-        nc.sync.dma_start(
-            out=raw[:].rearrange("p j t -> p (j t)")[:, 0:run], in_=xT.rearrange("(p j) t -> p (j t)", j=PACK)[:, 0:run]
-        )
-        for t0, n in ROW1_PIECES[1:]:
-            nc.sync.dma_start(out=raw[:, 1, t0 : t0 + n], in_=x_rows[:, 1, t0 : t0 + n])
+        for i, (t0, n) in enumerate(ROW0_PIECES):
+            nc.sync.dma_start(out=rows[0][:, t0 : t0 + n], in_=x_rows[:, 0, t0 : t0 + n])
+            if i == 0:
+                nc.sync.dma_start(offs_sb[:], offs)
+        for t0, n in ROW1_PIECES:
+            nc.sync.dma_start(out=rows[1][:, t0 : t0 + n], in_=x_rows[:, 1, t0 : t0 + n])
+        for j in (2, 3):
+            nc.sync.dma_start(out=rows[j][:], in_=x_rows[:, j, :])
         for g in range(4):
             nc.sync.dma_start(
                 out=ws_sb[32 * g : 32 * g + 4, :, :].bitcast(I32),
@@ -102,6 +88,11 @@ def tile_routed_moe_kernel(tc, xT, w_words, w_scales, b, gate, offs, pos1, pos2,
             )
         nc.sync.dma_start(out=w_sb[:], in_=w_words.rearrange("e a p n r -> p (e a) (n r)"))
         nc.sync.dma_start(out=b_sb[:], in_=b)
+        blocks = gate[1, 0, VECTOR_TOKENS:T].rearrange("(c p) -> c p", p=P)
+        for c0, c1 in ((0, 4), (4, 6)):
+            nc.sync.dma_start(out=gate2_rows[c0:c1, :], in_=blocks[c0:c1, :])
+        gate_bank = psum.tile([P, P], F32, name="bank")
+        nc.tensor.transpose(gate_bank[:], gate2_rows[:], ident[:])
         nc.sync.dma_start(pos1_sb[:], pos1)
         nc.sync.dma_start(pos2_sb[:], pos2)
         nc.sync.dma_start(out=gate1_sb[:], in_=gate[0])
@@ -110,41 +101,50 @@ def tile_routed_moe_kernel(tc, xT, w_words, w_scales, b, gate, offs, pos1, pos2,
         def slots_of(j0, n):
             return offs_sb[:, j0 // LIST : (j0 + n) // LIST]
 
-        first_high = first_pairs[:, :, 1, :].bitcast(BF16).rearrange("p i (n e) -> p i n e", e=2)
-        late_high = late_pairs[:, 1, :].bitcast(BF16).rearrange("p (n e) -> p n e", e=2)
+        def slot_pairs(j0, n, u):
+            return pairs[:, j0 // BLOCK : (j0 + n) // BLOCK, u, :]
 
-        nc.scalar.copy(out=row2[:, 0:ROW2_SCALAR], in_=raw[:, 2, 0:ROW2_SCALAR])
-        nc.vector.tensor_copy(out=row2[:, ROW2_SCALAR:ROW2_CUT], in_=raw[:, 2, ROW2_SCALAR:ROW2_CUT])
-        nc.vector.tensor_copy(out=row2[:, ROW2_CUT:T], in_=raw[:, 2, ROW2_CUT:T])
-        nc.gpsimd.tensor_copy(out=row3[:, 0:T], in_=raw3)
-        for e, window in enumerate((raw[:, 2, :], raw3)):
-            nc.vector.tensor_copy(out=late_high[:, 0:EARLY, e], in_=window.indirect(slots_of(HALF, EARLY)))
-        for e, window in enumerate((row2, row3)):
-            nc.scalar.activation(first_high[:, :, :, e], window[:].indirect(slots_of(0, 2 * PIECE)), COPY)
-        for e, window in enumerate((row2, row3)):
-            nc.scalar.activation(late_high[:, EARLY:HALF, e], window[:].indirect(slots_of(HALF + EARLY, HALF - EARLY)), COPY)
+        def gather_row(j, j0, n):
+            halves = slot_pairs(j0, n, j // 2).bitcast(BF16).rearrange("p b (n e) -> p b n e", e=2)
+            nc.scalar.activation(halves[:, :, :, j % 2], rows[j][:].indirect(slots_of(j0, n)), COPY)
 
-        for t0, n in ROW1_PIECES:
-            nc.vector.tensor_copy(
-                out=low[:, t0 : t0 + n].bitcast(BF16).rearrange("p (c i j) -> p c j i", i=4, j=2),
-                in_=raw[:, 0:2, t0 : t0 + n].rearrange("p j (c i) -> p c j i", i=4),
+        def round_row(copy, paired, j, t0, n):
+            halves = paired[:].bitcast(BF16).rearrange("p (t e) -> p t e", e=2)
+            copy(out=halves[:, t0 : t0 + n, j % 2], in_=rows[j][:, t0 : t0 + n])
+
+        def lay(copy, j0, n):
+            copy(
+                out=grouped[:, 2 * j0 : 2 * (j0 + n)].rearrange("p (b n u) -> p b n u", n=BLOCK, u=2),
+                in_=pairs[:, j0 // BLOCK : (j0 + n) // BLOCK, :, :].rearrange("p b u n -> p b n u"),
             )
-        for i in range(PIECES):
-            nc.vector.tensor_copy(out=pairs[i][:, 0, :], in_=low[:].indirect(slots_of(i * PIECE, PIECE)))
 
-        grouped = [first_grouped[:, 0, :], first_grouped[:, 1, :]] + [pairs[i].rearrange("p u n -> p (u n)") for i in range(2)]
-        for i in range(PIECES):
-            copy = nc.gpsimd.tensor_copy if i < 2 else nc.scalar.copy
-            copy(out=grouped[i].rearrange("p (n u) -> p n u", u=2), in_=pairs[i].rearrange("p u n -> p n u"))
+        for j, pieces in ((0, ROW0_PIECES), (1, ROW1_PIECES)):
+            for t0, n in pieces:
+                round_row(nc.vector.tensor_copy, low, j, t0, n)
+            gather_row(j, *SCALAR_LOW)
+        for j0, n in VECTOR_LOW:
+            nc.vector.tensor_copy(out=slot_pairs(j0, n, 0), in_=low[:].indirect(slots_of(j0, n)))
+        for j in (2, 3):
+            round_row(nc.gpsimd.tensor_copy, high, j, 0, T)
+        for j0, n in SCALAR_HIGH:
+            for j in (2, 3):
+                gather_row(j, j0, n)
+        gate2_cols = turns.tile([P, SCALAR_TOKENS // P], F32, name="gate2_cols", tag="row3")
+        nc.scalar.copy(out=gate2_cols[:], in_=gate_bank[:, 0 : SCALAR_TOKENS // P])
+        for j0, n in VECTOR_HIGH:
+            nc.vector.tensor_copy(out=slot_pairs(j0, n, 1), in_=high[:].indirect(slots_of(j0, n)))
+        for j0, n in GPSIMD_LAYS:
+            lay(nc.gpsimd.tensor_copy, j0, n)
+        for j0, n in SCALAR_LAYS:
+            lay(nc.scalar.copy, j0, n)
 
         y = turns.tile([P, SLOTS], F32, name="y", tag="turns", align_bytes=64)
         for_vector = []
         for j0, n in QUANTISE_PIECES:
-            c0 = j0 % PIECE
             nc.vector.quantize_mx(
                 out=s_words[:, j0 : j0 + n].bitcast(FP8X4),
                 scales=s_scales[:, j0 : j0 + n],
-                in_=grouped[j0 // PIECE][:, 2 * c0 : 2 * (c0 + n)].bitcast(BF16),
+                in_=grouped[:, 2 * j0 : 2 * (j0 + n)].bitcast(BF16),
             )
             for e in range(j0 // C, (j0 + n - 1) // C + 1):
                 lo, hi = max(j0, e * C), min(j0 + n, (e + 1) * C)

@@ -27,12 +27,15 @@ FLOPS = 2 * K * N * SLOTS
 BLOCK = 128
 ROW0_PIECES = ((0, 768), (768, 256))
 ROW1_PIECES = ((0, 512), (512, 512))
-SCALAR_LOW = (0, 512)
-VECTOR_LOW = ((512, 768), (1280, 768))
-SCALAR_HIGH = ((0, 256), (256, 512))
-VECTOR_HIGH = ((768, 512), (1280, 384), (1664, 384))
-GPSIMD_LAYS = ((0, 256), (256, 512))
-SCALAR_LAYS = ((768, 512), (1280, 384), (1664, 384))
+SCALAR_LOW = (0, 384)
+VECTOR_LOW = ((384, 896), (1280, 768))
+LOW_WINDOW = 1280
+SCALAR_ROW2 = (0, 896)
+ROW2_WINDOW = 1792
+SCALAR_ROW3 = ((0, 384), (384, 256), (640, 256))
+VECTOR_HIGH = ((896, 384), (1280, 384), (1664, 384))
+GPSIMD_LAYS = SCALAR_ROW3[:2]
+SCALAR_LAYS = ((640, 640), (1280, 384), (1664, 384))
 QUANTISE_PIECES = ((0, 256), (256, 256), (512, 512), (1024, 512), (1536, 256), (1792, 128), (1920, 128))
 VECTOR_EMPTIES = (3, 6)
 VECTOR_TOKENS = 256
@@ -51,9 +54,9 @@ def tile_routed_moe_kernel(tc, xT, w_words, w_scales, b, gate, offs, pos1, pos2,
         offs_sb = keep.tile([P, SLOTS // LIST], U16, name="offs_sb")
         pos1_sb = keep.tile([P, T // LIST], U16, name="pos1_sb")
         pos2_sb = keep.tile([P, T // LIST], U16, name="pos2_sb")
-        rows = [keep.tile([P, T], F32, name="row%d" % j) for j in range(PACK - 1)]
+        rows = [keep.tile([P, ROW2_WINDOW if j == 2 else T], F32, name="row%d" % j) for j in range(PACK - 1)]
         rows.append(turns.tile([P, T], F32, name="row3", tag="row3"))
-        low = keep.tile([P, T], U32, name="low", align_bytes=64)
+        low = keep.tile([P, LOW_WINDOW], U32, name="low", align_bytes=64)
         high = keep.tile([P, T], U32, name="high", align_bytes=64)
         pairs = turns.tile([P, SLOTS // BLOCK, 2, BLOCK], U32, name="pairs", tag="turns", align_bytes=64)
         grouped = keep.tile([P, 2 * SLOTS], U32, name="grouped", align_bytes=64)
@@ -70,6 +73,8 @@ def tile_routed_moe_kernel(tc, xT, w_words, w_scales, b, gate, offs, pos1, pos2,
         gate2_rows = keep.tile([P, P], F32, name="gate2_rows")
         nc.vector.memset(gate2_rows[:, 0 : P // 2], 0.0)
         nc.scalar.copy(out=gate2_rows[:, P // 2 : P], in_=gate2_rows[:, 0 : P // 2])
+        nc.vector.memset(low[:, T:LOW_WINDOW].bitcast(I32), 0)
+        nc.vector.memset(rows[2][:, T:ROW2_WINDOW], 0.0)
         nc.vector.memset(ws_sb[:].rearrange("p e n -> p (e n)").bitcast(I32), 0)
 
         x_rows = xT.rearrange("(p j) t -> p j t", j=PACK)
@@ -80,7 +85,7 @@ def tile_routed_moe_kernel(tc, xT, w_words, w_scales, b, gate, offs, pos1, pos2,
         for t0, n in ROW1_PIECES:
             nc.sync.dma_start(out=rows[1][:, t0 : t0 + n], in_=x_rows[:, 1, t0 : t0 + n])
         for j in (2, 3):
-            nc.sync.dma_start(out=rows[j][:], in_=x_rows[:, j, :])
+            nc.sync.dma_start(out=rows[j][:, 0:T], in_=x_rows[:, j, :])
         for g in range(4):
             nc.sync.dma_start(
                 out=ws_sb[32 * g : 32 * g + 4, :, :].bitcast(I32),
@@ -126,9 +131,9 @@ def tile_routed_moe_kernel(tc, xT, w_words, w_scales, b, gate, offs, pos1, pos2,
             nc.vector.tensor_copy(out=slot_pairs(j0, n, 0), in_=low[:].indirect(slots_of(j0, n)))
         for j in (2, 3):
             round_row(nc.gpsimd.tensor_copy, high, j, 0, T)
-        for j0, n in SCALAR_HIGH:
-            for j in (2, 3):
-                gather_row(j, j0, n)
+        gather_row(2, *SCALAR_ROW2)
+        for j0, n in SCALAR_ROW3:
+            gather_row(3, j0, n)
         gate2_cols = turns.tile([P, SCALAR_TOKENS // P], F32, name="gate2_cols", tag="row3")
         nc.scalar.copy(out=gate2_cols[:], in_=gate_bank[:, 0 : SCALAR_TOKENS // P])
         for j0, n in VECTOR_HIGH:

@@ -32,10 +32,10 @@ VECTOR_LOW = ((384, 896), (1280, 768))
 LOW_WINDOW = 1280
 SCALAR_ROW2 = (0, 896)
 ROW2_WINDOW = 1792
-SCALAR_ROW3 = ((0, 384), (384, 256), (640, 256))
+SCALAR_ROW3 = ((0, 384), (384, 384), (768, 128))
 VECTOR_HIGH = ((896, 384), (1280, 384), (1664, 384))
 GPSIMD_LAYS = SCALAR_ROW3[:2]
-SCALAR_LAYS = ((640, 640), (1280, 384), (1664, 384))
+SCALAR_LAYS = ((768, 512), (1280, 384), (1664, 384))
 QUANTISE_PIECES = ((0, 256), (256, 256), (512, 512), (1024, 512), (1536, 256), (1792, 128), (1920, 128))
 VECTOR_EMPTIES = (3, 6)
 VECTOR_TOKENS = 256

@@ -24,18 +24,19 @@ MULT = mybir.AluOpType.mult
 
 FLOPS = 2 * K * N * SLOTS
 
-BLOCK = 128
+BLOCK = 64
 ROW0_PIECES = ((0, 768), (768, 256))
-ROW1_PIECES = ((0, 512), (512, 512))
+ROW1_PIECES = ((0, 512), (512, 256), (768, 256))
+ROW2_PIECES = ((0, 512), (512, 512))
 SCALAR_LOW = (0, 384)
 VECTOR_LOW = ((384, 896), (1280, 768))
 LOW_WINDOW = 1280
-SCALAR_ROW2 = (0, 896)
-ROW2_WINDOW = 1792
-SCALAR_ROW3 = ((0, 384), (384, 384), (768, 128))
-VECTOR_HIGH = ((896, 384), (1280, 384), (1664, 384))
-GPSIMD_LAYS = SCALAR_ROW3[:2]
-SCALAR_LAYS = ((768, 512), (1280, 384), (1664, 384))
+SCALAR_ROW2 = (0, 832)
+ROW2_WINDOW = 1664
+SCALAR_ROW3 = ((0, 384), (384, 448))
+VECTOR_HIGH = ((832, 448), (1280, 384), (1664, 384))
+GPSIMD_LAYS = SCALAR_ROW3
+SCALAR_LAYS = VECTOR_HIGH
 QUANTISE_PIECES = ((0, 256), (256, 256), (512, 512), (1024, 512), (1536, 256), (1792, 128), (1920, 128))
 VECTOR_EMPTIES = (3, 6)
 VECTOR_TOKENS = 256
@@ -84,8 +85,9 @@ def tile_routed_moe_kernel(tc, xT, w_words, w_scales, b, gate, offs, pos1, pos2,
                 nc.sync.dma_start(offs_sb[:], offs)
         for t0, n in ROW1_PIECES:
             nc.sync.dma_start(out=rows[1][:, t0 : t0 + n], in_=x_rows[:, 1, t0 : t0 + n])
-        for j in (2, 3):
-            nc.sync.dma_start(out=rows[j][:, 0:T], in_=x_rows[:, j, :])
+        for t0, n in ROW2_PIECES:
+            nc.sync.dma_start(out=rows[2][:, t0 : t0 + n], in_=x_rows[:, 2, t0 : t0 + n])
+        nc.sync.dma_start(out=rows[3][:], in_=x_rows[:, 3, :])
         for g in range(4):
             nc.sync.dma_start(
                 out=ws_sb[32 * g : 32 * g + 4, :, :].bitcast(I32),
@@ -129,8 +131,9 @@ def tile_routed_moe_kernel(tc, xT, w_words, w_scales, b, gate, offs, pos1, pos2,
             gather_row(j, *SCALAR_LOW)
         for j0, n in VECTOR_LOW:
             nc.vector.tensor_copy(out=slot_pairs(j0, n, 0), in_=low[:].indirect(slots_of(j0, n)))
-        for j in (2, 3):
-            round_row(nc.gpsimd.tensor_copy, high, j, 0, T)
+        for t0, n in ROW2_PIECES:
+            round_row(nc.gpsimd.tensor_copy, high, 2, t0, n)
+        round_row(nc.gpsimd.tensor_copy, high, 3, 0, T)
         gather_row(2, *SCALAR_ROW2)
         for j0, n in SCALAR_ROW3:
             gather_row(3, j0, n)

@@ -28,17 +28,17 @@ BLOCK = 64
 ROW0_PIECES = ((0, 768), (768, 256))
 ROW1_PIECES = ((0, 512), (512, 256), (768, 256))
 ROW2_PIECES = ((0, 512), (512, 512))
-SCALAR_LOW = (0, 384)
-VECTOR_LOW = ((384, 896), (1280, 768))
-LOW_WINDOW = 1280
+SCALAR_LOW = (0, 448)
+LOW_WINDOW = 1120
+VECTOR_LOW = ((448, 768, T), (1216, 832, LOW_WINDOW))
 SCALAR_ROW2 = (0, 832)
 ROW2_WINDOW = 1664
 SCALAR_ROW3 = ((0, 384), (384, 448))
 VECTOR_HIGH = ((832, 448), (1280, 384), (1664, 384))
 GPSIMD_LAYS = SCALAR_ROW3
 SCALAR_LAYS = VECTOR_HIGH
-QUANTISE_PIECES = ((0, 256), (256, 256), (512, 512), (1024, 512), (1536, 256), (1792, 128), (1920, 128))
-VECTOR_EMPTIES = (3, 6)
+QUANTISE_PIECES = ((0, 512), (512, 512), (1024, 512), (1536, 256), (1792, 128), (1920, 128))
+VECTOR_EMPTIES = (5,)
 VECTOR_TOKENS = 256
 SCALAR_TOKENS = T - VECTOR_TOKENS
 SCALAR_STEPS = ((512, 384, 0), (256, 256, 2), (896, 128, 4))
@@ -74,7 +74,6 @@ def tile_routed_moe_kernel(tc, xT, w_words, w_scales, b, gate, offs, pos1, pos2,
         gate2_rows = keep.tile([P, P], F32, name="gate2_rows")
         nc.vector.memset(gate2_rows[:, 0 : P // 2], 0.0)
         nc.scalar.copy(out=gate2_rows[:, P // 2 : P], in_=gate2_rows[:, 0 : P // 2])
-        nc.vector.memset(low[:, T:LOW_WINDOW].bitcast(I32), 0)
         nc.vector.memset(rows[2][:, T:ROW2_WINDOW], 0.0)
         nc.vector.memset(ws_sb[:].rearrange("p e n -> p (e n)").bitcast(I32), 0)
 
@@ -129,8 +128,9 @@ def tile_routed_moe_kernel(tc, xT, w_words, w_scales, b, gate, offs, pos1, pos2,
             for t0, n in pieces:
                 round_row(nc.vector.tensor_copy, low, j, t0, n)
             gather_row(j, *SCALAR_LOW)
-        for j0, n in VECTOR_LOW:
-            nc.vector.tensor_copy(out=slot_pairs(j0, n, 0), in_=low[:].indirect(slots_of(j0, n)))
+        nc.gpsimd.tensor_copy(out=low[:, T:LOW_WINDOW], in_=low[:, 2 * T - LOW_WINDOW : T])
+        for j0, n, columns in VECTOR_LOW:
+            nc.vector.tensor_copy(out=slot_pairs(j0, n, 0), in_=low[:, 0:columns].indirect(slots_of(j0, n)))
         for t0, n in ROW2_PIECES:
             round_row(nc.gpsimd.tensor_copy, high, 2, t0, n)
         round_row(nc.gpsimd.tensor_copy, high, 3, 0, T)

@@ -31,14 +31,14 @@ ROW2_PIECES = ((0, 512), (512, 512))
 SCALAR_LOW = (0, 448)
 LOW_WINDOW = 1120
 VECTOR_LOW = ((448, 768, T), (1216, 832, LOW_WINDOW))
-SCALAR_ROW2 = (0, 832)
-ROW2_WINDOW = 1664
-SCALAR_ROW3 = ((0, 384), (384, 448))
-VECTOR_HIGH = ((832, 448), (1280, 384), (1664, 384))
-GPSIMD_LAYS = SCALAR_ROW3
-SCALAR_LAYS = VECTOR_HIGH
-QUANTISE_PIECES = ((0, 512), (512, 512), (1024, 512), (1536, 256), (1792, 128), (1920, 128))
-VECTOR_EMPTIES = (5,)
+SCALAR_ROW2 = (0, 896)
+ROW2_WINDOW = 1792
+SCALAR_ROW3 = ((0, 384), (384, 384), (768, 128))
+VECTOR_HIGH = ((896, 384), (1280, 384), (1664, 384))
+GPSIMD_LAYS = SCALAR_ROW3[:2]
+SCALAR_LAYS = ((768, 512), (1280, 384), (1664, 384))
+QUANTISE_PIECES = ((0, 256), (256, 256), (512, 512), (1024, 512), (1536, 256), (1792, 128), (1920, 128))
+VECTOR_EMPTIES = (3, 6)
 VECTOR_TOKENS = 256
 SCALAR_TOKENS = T - VECTOR_TOKENS
 SCALAR_STEPS = ((512, 384, 0), (256, 256, 2), (896, 128, 4))

@@ -26,17 +26,17 @@ FLOPS = 2 * K * N * SLOTS
 
 BLOCK = 64
 ROW0_PIECES = ((0, 768), (768, 256))
-ROW1_PIECES = ((0, 512), (512, 256), (768, 256))
+ROW1_PIECES = ((0, 384), (384, 384), (768, 256))
 ROW2_PIECES = ((0, 512), (512, 512))
 SCALAR_LOW = (0, 448)
 LOW_WINDOW = 1120
 VECTOR_LOW = ((448, 768, T), (1216, 832, LOW_WINDOW))
 SCALAR_ROW2 = (0, 896)
 ROW2_WINDOW = 1792
-SCALAR_ROW3 = ((0, 384), (384, 384), (768, 128))
+SCALAR_ROW3 = ((0, 384), (384, 320), (704, 192))
 VECTOR_HIGH = ((896, 384), (1280, 384), (1664, 384))
 GPSIMD_LAYS = SCALAR_ROW3[:2]
-SCALAR_LAYS = ((768, 512), (1280, 384), (1664, 384))
+SCALAR_LAYS = ((704, 576), (1280, 384), (1664, 384))
 QUANTISE_PIECES = ((0, 256), (256, 256), (512, 512), (1024, 512), (1536, 256), (1792, 128), (1920, 128))
 VECTOR_EMPTIES = (3, 6)
 VECTOR_TOKENS = 256

@@ -27,7 +27,7 @@ FLOPS = 2 * K * N * SLOTS
 BLOCK = 64
 ROW0_PIECES = ((0, 768), (768, 256))
 ROW1_PIECES = ((0, 384), (384, 384), (768, 256))
-ROW2_PIECES = ((0, 512), (512, 512))
+ROW2_PIECES = ((0, 768), (768, 256))
 SCALAR_LOW = (0, 448)
 LOW_WINDOW = 1120
 VECTOR_LOW = ((448, 768, T), (1216, 832, LOW_WINDOW))
@@ -75,6 +75,7 @@ def tile_routed_moe_kernel(tc, xT, w_words, w_scales, b, gate, offs, pos1, pos2,
         nc.vector.memset(gate2_rows[:, 0 : P // 2], 0.0)
         nc.scalar.copy(out=gate2_rows[:, P // 2 : P], in_=gate2_rows[:, 0 : P // 2])
         nc.vector.memset(rows[2][:, T:ROW2_WINDOW], 0.0)
+        nc.vector.memset(low[:, T:LOW_WINDOW].bitcast(I32), 0)
         nc.vector.memset(ws_sb[:].rearrange("p e n -> p (e n)").bitcast(I32), 0)
 
         x_rows = xT.rearrange("(p j) t -> p j t", j=PACK)
@@ -128,7 +129,6 @@ def tile_routed_moe_kernel(tc, xT, w_words, w_scales, b, gate, offs, pos1, pos2,
             for t0, n in pieces:
                 round_row(nc.vector.tensor_copy, low, j, t0, n)
             gather_row(j, *SCALAR_LOW)
-        nc.gpsimd.tensor_copy(out=low[:, T:LOW_WINDOW], in_=low[:, 2 * T - LOW_WINDOW : T])
         for j0, n, columns in VECTOR_LOW:
             nc.vector.tensor_copy(out=slot_pairs(j0, n, 0), in_=low[:, 0:columns].indirect(slots_of(j0, n)))
         for t0, n in ROW2_PIECES:

@@ -27,7 +27,7 @@ FLOPS = 2 * K * N * SLOTS
 BLOCK = 64
 ROW0_PIECES = ((0, 768), (768, 256))
 ROW1_PIECES = ((0, 384), (384, 384), (768, 256))
-ROW2_PIECES = ((0, 768), (768, 256))
+ROW2_PIECES = ((0, 640), (640, 384))
 SCALAR_LOW = (0, 448)
 LOW_WINDOW = 1120
 VECTOR_LOW = ((448, 768, T), (1216, 832, LOW_WINDOW))

from contextlib import ExitStack

import concourse.mybir as mybir
from concourse.masks import make_identity

K, T, E, C, N = 512, 1024, 8, 256, 128
SLOTS = E * C
P = 128
PACK = 4
LIST = 16

F32 = mybir.dt.float32
BF16 = mybir.dt.bfloat16
U32 = mybir.dt.uint32
I32 = mybir.dt.int32
U16 = mybir.dt.uint16
U8 = mybir.dt.uint8
FP8X4 = mybir.dt.float8_e4m3fn_x4
COPY = mybir.ActivationFunctionType.Copy
RELU = mybir.ActivationFunctionType.Relu
ADD = mybir.AluOpType.add
MAX = mybir.AluOpType.max
MULT = mybir.AluOpType.mult

FLOPS = 2 * K * N * SLOTS

BLOCK = 64
ROW0_PIECES = ((0, 768), (768, 256))
ROW1_PIECES = ((0, 384), (384, 384), (768, 256))
ROW2_PIECES = ((0, 640), (640, 384))
SCALAR_LOW = (0, 448)
LOW_WINDOW = 1120
VECTOR_LOW = ((448, 768, T), (1216, 832, LOW_WINDOW))
SCALAR_ROW2 = (0, 896)
ROW2_WINDOW = 1792
SCALAR_ROW3 = ((0, 384), (384, 320), (704, 192))
VECTOR_HIGH = ((896, 384), (1280, 384), (1664, 384))
GPSIMD_LAYS = SCALAR_ROW3[:2]
SCALAR_LAYS = ((704, 576), (1280, 384), (1664, 384))
QUANTISE_PIECES = ((0, 256), (256, 256), (512, 512), (1024, 512), (1536, 256), (1792, 128), (1920, 128))
VECTOR_EMPTIES = (3, 6)
VECTOR_TOKENS = 256
SCALAR_TOKENS = T - VECTOR_TOKENS
SCALAR_STEPS = ((512, 384, 0), (256, 256, 2), (896, 128, 4))
FINISH = ((512, 256, (512, 256)), (256, 256, (0, 512)), (768, 128, None), (896, 128, (768, 256)))


def tile_routed_moe_kernel(tc, xT, w_words, w_scales, b, gate, offs, pos1, pos2, out):
    nc = tc.nc
    with ExitStack() as ctx:
        keep = ctx.enter_context(tc.tile_pool(name="keep", bufs=1))
        turns = ctx.enter_context(tc.tile_pool(name="turns", bufs=1))
        psum = ctx.enter_context(tc.psum_pool(name="psum", bufs=8))

        offs_sb = keep.tile([P, SLOTS // LIST], U16, name="offs_sb")
        pos1_sb = keep.tile([P, T // LIST], U16, name="pos1_sb")
        pos2_sb = keep.tile([P, T // LIST], U16, name="pos2_sb")
        rows = [keep.tile([P, ROW2_WINDOW if j == 2 else T], F32, name="row%d" % j) for j in range(PACK - 1)]
        rows.append(turns.tile([P, T], F32, name="row3", tag="row3"))
        low = keep.tile([P, LOW_WINDOW], U32, name="low", align_bytes=64)
        high = keep.tile([P, T], U32, name="high", align_bytes=64)
        pairs = turns.tile([P, SLOTS // BLOCK, 2, BLOCK], U32, name="pairs", tag="turns", align_bytes=64)
        grouped = keep.tile([P, 2 * SLOTS], U32, name="grouped", align_bytes=64)
        s_words = keep.tile([P, SLOTS], U32, name="s_words", align_bytes=64)
        s_scales = keep.tile([P, SLOTS], U8, name="s_scales", align_bytes=64)
        w_sb = keep.tile([P, E, N * PACK], U8, name="w_sb", align_bytes=64)
        ws_sb = keep.tile([P, E, N], U8, name="ws_sb", align_bytes=64)
        b_sb = keep.tile([P, E], F32, name="b_sb")
        gate1_sb = keep.tile([P, T], F32, name="gate1_sb")
        gate2_sb = keep.tile([P, VECTOR_TOKENS], F32, name="gate2_sb")
        ident = keep.tile([P, P], F32, name="ident")
        make_identity(nc, ident[:])

        gate2_rows = keep.tile([P, P], F32, name="gate2_rows")
        nc.vector.memset(gate2_rows[:, 0 : P // 2], 0.0)
        nc.scalar.copy(out=gate2_rows[:, P // 2 : P], in_=gate2_rows[:, 0 : P // 2])
        nc.vector.memset(rows[2][:, T:ROW2_WINDOW], 0.0)
        nc.vector.memset(low[:, T:LOW_WINDOW].bitcast(I32), 0)
        nc.vector.memset(ws_sb[:].rearrange("p e n -> p (e n)").bitcast(I32), 0)

        x_rows = xT.rearrange("(p j) t -> p j t", j=PACK)
        for i, (t0, n) in enumerate(ROW0_PIECES):
            nc.sync.dma_start(out=rows[0][:, t0 : t0 + n], in_=x_rows[:, 0, t0 : t0 + n])
            if i == 0:
                nc.sync.dma_start(offs_sb[:], offs)
        for t0, n in ROW1_PIECES:
            nc.sync.dma_start(out=rows[1][:, t0 : t0 + n], in_=x_rows[:, 1, t0 : t0 + n])
        for t0, n in ROW2_PIECES:
            nc.sync.dma_start(out=rows[2][:, t0 : t0 + n], in_=x_rows[:, 2, t0 : t0 + n])
        nc.sync.dma_start(out=rows[3][:], in_=x_rows[:, 3, :])
        for g in range(4):
            nc.sync.dma_start(
                out=ws_sb[32 * g : 32 * g + 4, :, :].bitcast(I32),
                in_=w_scales[:, 0, 4 * g : 4 * g + 4, :].rearrange("e q n -> q e n").bitcast(I32),
            )
        nc.sync.dma_start(out=w_sb[:], in_=w_words.rearrange("e a p n r -> p (e a) (n r)"))
        nc.sync.dma_start(out=b_sb[:], in_=b)
        blocks = gate[1, 0, VECTOR_TOKENS:T].rearrange("(c p) -> c p", p=P)
        for c0, c1 in ((0, 4), (4, 6)):
            nc.sync.dma_start(out=gate2_rows[c0:c1, :], in_=blocks[c0:c1, :])
        gate_bank = psum.tile([P, P], F32, name="bank")
        nc.tensor.transpose(gate_bank[:], gate2_rows[:], ident[:])
        nc.sync.dma_start(pos1_sb[:], pos1)
        nc.sync.dma_start(pos2_sb[:], pos2)
        nc.sync.dma_start(out=gate1_sb[:], in_=gate[0])
        nc.sync.dma_start(out=gate2_sb[:], in_=gate[1, :, 0:VECTOR_TOKENS])

        def slots_of(j0, n):
            return offs_sb[:, j0 // LIST : (j0 + n) // LIST]

        def slot_pairs(j0, n, u):
            return pairs[:, j0 // BLOCK : (j0 + n) // BLOCK, u, :]

        def gather_row(j, j0, n):
            halves = slot_pairs(j0, n, j // 2).bitcast(BF16).rearrange("p b (n e) -> p b n e", e=2)
            nc.scalar.activation(halves[:, :, :, j % 2], rows[j][:].indirect(slots_of(j0, n)), COPY)

        def round_row(copy, paired, j, t0, n):
            halves = paired[:].bitcast(BF16).rearrange("p (t e) -> p t e", e=2)
            copy(out=halves[:, t0 : t0 + n, j % 2], in_=rows[j][:, t0 : t0 + n])

        def lay(copy, j0, n):
            copy(
                out=grouped[:, 2 * j0 : 2 * (j0 + n)].rearrange("p (b n u) -> p b n u", n=BLOCK, u=2),
                in_=pairs[:, j0 // BLOCK : (j0 + n) // BLOCK, :, :].rearrange("p b u n -> p b n u"),
            )

        for j, pieces in ((0, ROW0_PIECES), (1, ROW1_PIECES)):
            for t0, n in pieces:
                round_row(nc.vector.tensor_copy, low, j, t0, n)
            gather_row(j, *SCALAR_LOW)
        for j0, n, columns in VECTOR_LOW:
            nc.vector.tensor_copy(out=slot_pairs(j0, n, 0), in_=low[:, 0:columns].indirect(slots_of(j0, n)))
        for t0, n in ROW2_PIECES:
            round_row(nc.gpsimd.tensor_copy, high, 2, t0, n)
        round_row(nc.gpsimd.tensor_copy, high, 3, 0, T)
        gather_row(2, *SCALAR_ROW2)
        for j0, n in SCALAR_ROW3:
            gather_row(3, j0, n)
        gate2_cols = turns.tile([P, SCALAR_TOKENS // P], F32, name="gate2_cols", tag="row3")
        nc.scalar.copy(out=gate2_cols[:], in_=gate_bank[:, 0 : SCALAR_TOKENS // P])
        for j0, n in VECTOR_HIGH:
            nc.vector.tensor_copy(out=slot_pairs(j0, n, 1), in_=high[:].indirect(slots_of(j0, n)))
        for j0, n in GPSIMD_LAYS:
            lay(nc.gpsimd.tensor_copy, j0, n)
        for j0, n in SCALAR_LAYS:
            lay(nc.scalar.copy, j0, n)

        y = turns.tile([P, SLOTS], F32, name="y", tag="turns", align_bytes=64)
        for_vector = []
        for j0, n in QUANTISE_PIECES:
            nc.vector.quantize_mx(
                out=s_words[:, j0 : j0 + n].bitcast(FP8X4),
                scales=s_scales[:, j0 : j0 + n],
                in_=grouped[:, 2 * j0 : 2 * (j0 + n)].bitcast(BF16),
            )
            for e in range(j0 // C, (j0 + n - 1) // C + 1):
                lo, hi = max(j0, e * C), min(j0 + n, (e + 1) * C)
                acc = psum.tile([N, hi - lo], F32, name="bank")
                nc.tensor.matmul_mx(
                    out=acc[:],
                    lhsT=w_sb[:, e, :].bitcast(FP8X4),
                    lhsT_scale=ws_sb[:, e, :],
                    rhs=s_words[:, lo:hi].bitcast(FP8X4),
                    rhs_scale=s_scales[:, lo:hi],
                    start=True,
                    stop=True,
                )
                if e in VECTOR_EMPTIES:
                    for_vector.append((e, acc))
                else:
                    nc.scalar.activation(y[:, lo:hi], acc[:], RELU, bias=b_sb[:, e : e + 1])
        for e, acc in for_vector:
            nc.vector.tensor_scalar(y[:, e * C : (e + 1) * C], acc[:], b_sb[:, e : e + 1], 0.0, ADD, MAX)

        def results(pos_sb, t0, n):
            return y[:].indirect(pos_sb[:, t0 // LIST : (t0 + n) // LIST])

        first = keep.tile([P, T], F32, name="first")
        nc.vector.tensor_tensor(first[:], results(pos1_sb, 0, T), gate1_sb[:], MULT)
        second = keep.tile([P, T], F32, name="second")
        nc.vector.tensor_tensor(second[:, 0:VECTOR_TOKENS], results(pos2_sb, 0, VECTOR_TOKENS), gate2_sb[:], MULT)
        total = keep.tile([P, T], F32, name="total")
        nc.gpsimd.tensor_tensor(total[:, 0:VECTOR_TOKENS], first[:, 0:VECTOR_TOKENS], second[:, 0:VECTOR_TOKENS], ADD)

        order = [t0 for b0, n, stored in FINISH for t0 in range(b0, b0 + n, P)]
        turned = {}
        weighed = keep.tile([P, T], F32, name="weighed")
        backs = {}
        done = 0
        for g0, gn, count in SCALAR_STEPS:
            nc.scalar.activation(second[:, g0 : g0 + gn], results(pos2_sb, g0, gn), COPY)
            for b0 in range(g0, g0 + gn, 2 * P):
                width = min(2 * P, g0 + gn - b0)
                bank = psum.tile([P, width], F32, name="bank")
                for c0 in range(0, width, P):
                    nc.tensor.transpose(bank[:, c0 : c0 + P], second[:, b0 + c0 : b0 + c0 + P], ident[:])
                    turned[b0 + c0] = bank[:, c0 : c0 + P]
            for t0 in order[done : done + count]:
                c = (t0 - VECTOR_TOKENS) // P
                nc.scalar.activation(weighed[:, t0 : t0 + P], turned[t0], COPY, scale=gate2_cols[:, c : c + 1])
                for b0, n, stored in FINISH:
                    if b0 <= t0 < b0 + n:
                        if t0 == b0:
                            backs[b0] = psum.tile([P, n], F32, name="bank")
                        nc.tensor.transpose(backs[b0][:, t0 - b0 : t0 - b0 + P], weighed[:, t0 : t0 + P], ident[:])
                        if t0 + P == b0 + n:
                            nc.vector.tensor_tensor(total[:, b0 : b0 + n], backs[b0][:], first[:, b0 : b0 + n], ADD)
                            if stored is not None:
                                s0, sn = stored
                                nc.sync.dma_start(out=out[:, s0 : s0 + sn], in_=total[:, s0 : s0 + sn])
            done += count
